import numpy as np
import ml_dtypes


def mxq(x, axis, fmt="e4m3"):
    dtype, down = {"e4m3": (ml_dtypes.float8_e4m3fn, 7), "e5m2": (ml_dtypes.float8_e5m2, 14)}[fmt]
    v = np.moveaxis(np.asarray(x, np.float32).astype(ml_dtypes.bfloat16).astype(np.float64), axis, -1)
    blocks = v.reshape(v.shape[:-1] + (-1, 32))
    amax = np.abs(blocks).max(-1, keepdims=True)
    byte = np.maximum(np.where(amax > 0, np.frexp(amax)[1] - 1 + 127, 0) - down, 1)
    scale = np.exp2(byte - 127.0)
    codes = (blocks / scale).astype(np.float32).astype(dtype).astype(np.float64)
    return np.moveaxis((codes * scale).reshape(v.shape), -1, axis)


WIDE = False


def mx_kscale(k):
    if not WIDE:
        return np.ones(k)
    levels = np.array([10, -10, 5, -5, 0])
    if k % 512:
        return np.exp2(np.random.permutation(np.resize(levels, k // 32))).repeat(32)
    a = np.empty((k // 512, 16))
    for p in range(k // 512):
        a[p, :8] = np.random.permutation(np.resize(levels, 8))
        for g in range(8):
            far = levels[np.abs(levels - a[p, g]) >= 10]
            a[p, g + 8] = far[np.random.randint(len(far))]
    return np.exp2(a.ravel()).repeat(32)


def f64(x):
    return np.asarray(x).astype(np.float64)


def striped(idx):
    return np.tile(idx.reshape(-1, 16).T, (8, 1)).astype(np.uint16)


def unstriped(offs):
    return offs[:16].T.reshape(-1).astype(np.int64)


def striped8(idx):
    return np.concatenate([x.reshape(-1, 16).T for x in idx]).astype(np.uint16)


def runs(offs, k):
    lists = np.stack([offs[16 * r : 16 * r + 16].T.reshape(-1) for r in range(8)]).astype(np.int64)
    return lists[np.arange(k) % 512 // 64]


def pack_weight(w):
    k, n = w.shape
    w = f64(np.asarray(w, np.float32).astype(ml_dtypes.bfloat16)).reshape(k // 32, 32, n)
    amax = np.abs(w).max(1)
    byte = np.clip(np.where(amax > 0, np.frexp(amax)[1] - 1 + 127 - 7, 1), 1, 254)
    scaled = (w * np.exp2(127.0 - byte)[:, None, :]).reshape(k, n).astype(np.float32)
    words = np.ascontiguousarray(scaled.reshape(k // 512, 128, 4, n).transpose(0, 1, 3, 2)).astype(ml_dtypes.float8_e4m3fn).view(np.uint8)
    return words, np.ascontiguousarray(byte.astype(np.uint8).reshape(k // 512, 16, n))


def unpack_weight(words, scales):
    g, p, n, _ = words.shape
    vals = np.ascontiguousarray(words).view(ml_dtypes.float8_e4m3fn).astype(np.float64) * np.repeat(np.exp2(scales.astype(np.float64) - 127.0), 8, axis=1)[..., None]
    return vals.transpose(0, 1, 3, 2).reshape(g * 512, n)

def planes(y):
    n, m = y.shape
    v = y.astype(np.float32).astype(ml_dtypes.bfloat16).astype(np.float64).reshape(n // 32, 32, m)
    top = np.abs(v).max(1)
    byte = np.clip(np.where(top > 0, np.frexp(top)[1] - 1 + 127 - 7, 1), 1, 254)
    codes = (v * np.exp2(127.0 - byte)[:, None, :]).reshape(n, m).astype(np.float32).astype(ml_dtypes.float8_e4m3fn).view(np.uint8)
    words = codes.reshape(n // 512, 128, 4, m).transpose(0, 1, 3, 2)
    return np.ascontiguousarray(words), np.ascontiguousarray(byte.astype(np.uint8).reshape(n // 512, 16, m))


K, T, S, N, G, H = 512, 2048, 512, 512, 2048, 512


def setup_inputs():
    n = np.random.standard_normal
    s = mx_kscale(K)[:, None]
    u = mx_kscale(H)
    packed_xT = pack_weight(n((K, T)) * s)
    packed_dT = pack_weight(n((K, G)) / s)
    packed_w1 = pack_weight(n((H, N)) / np.sqrt(H) / u[:, None])
    return {
        "x_words": packed_xT[0],
        "x_scales": packed_xT[1],
        "d_words": packed_dT[0],
        "d_scales": packed_dT[1],
        "kb": (0.5 * n((H, 1))).astype(np.float32),
        "gn": (np.random.uniform(0.5, 1.5, (H, 1)) * u[:, None]).astype(np.float32),
        "w1_words": packed_w1[0],
        "w1_scales": packed_w1[1],
        "offs": striped(np.random.permutation(T)[:S]),
        "kidx": striped8(np.random.randint(0, G, (8, H))),
    }


def reference(x_words, x_scales, d_words, d_scales, kb, gn, w1_words, w1_scales, offs, kidx):
    d_kidx = unpack_weight(d_words, d_scales)[np.arange(K)[:, None], runs(kidx, K)]
    xq = unpack_weight(x_words, x_scales)[:, unstriped(offs)]
    s = 0.0625 * (d_kidx.T @ xq) + f64(kb)
    z = f64(gn) * np.tanh(s)
    out_0 = unpack_weight(w1_words, w1_scales).T @ mxq(z, 0, "e4m3")
    return (out_0,) + planes(out_0)

@@ -1,0 +1,174 @@
+from contextlib import ExitStack
+
+import concourse.mybir as mybir
+
+F32 = mybir.dt.float32
+BF16 = mybir.dt.bfloat16
+I32 = mybir.dt.int32
+U32 = mybir.dt.uint32
+U16 = mybir.dt.uint16
+U8 = mybir.dt.uint8
+FP8X4 = mybir.dt.float8_e4m3fn_x4
+ACT = mybir.ActivationFunctionType
+ALU = mybir.AluOpType
+
+P = 128
+PACK = 4
+TABLE = 2048
+PICKED = 512
+HALF = 256
+QUARTER = 128
+FLOPS = 2 * 2 * 512 * 512 * 512
+
+
+def deal(nc, dst, src, run):
+    nc.vector.tensor_copy(
+        out=dst.rearrange("p (t c i) -> p c t i", t=PACK, i=run),
+        in_=src.rearrange("p (c i t) -> p c t i", t=PACK, i=run),
+    )
+
+
+def tile_picked_sigattn_tanh_po_kernel(
+    tc, x_words, x_scales, d_words, d_scales, kb, gn, w1_words, w1_scales, offs, kidx, out_0, out_1, out_2
+):
+    nc = tc.nc
+    with ExitStack() as ctx:
+        sb = ctx.enter_context(tc.tile_pool(name="sb", bufs=1))
+        ps = ctx.enter_context(tc.psum_pool(name="ps", bufs=1))
+
+        def tile(name, shape, dtype, tag=None):
+            return sb.tile(shape, dtype, name=name, tag=tag or name, align_bytes=64)
+
+        kidx_sb = sb.tile([P, PICKED // 16], U16, name="kidx_sb")
+        offs_sb = sb.tile([P, PICKED // 16], U16, name="offs_sb")
+        d_scale_table = tile("d_scale_table", [P, TABLE], U8)
+        x_scale_table = tile("x_scale_table", [P, TABLE], U8)
+        d_word_table = tile("d_word_table", [P, TABLE], U32)
+        x_word_table = tile("x_word_table", [P, TABLE], U32)
+        w_word_in = tile("w_word_in", [P, PICKED], U32)
+        w_scale_in = tile("w_scale_in", [P, PICKED], U8)
+        score_scales = tile("score_scales", [P, 2 * PICKED], U8)
+        kb_sb = tile("kb_sb", [P, PACK], F32)
+        gn_sb = tile("gn_sb", [P, PACK], F32)
+
+        nc.vector.memset(d_scale_table[:].bitcast(I32), 0)
+        nc.vector.memset(x_scale_table[:].bitcast(I32), 0)
+        nc.vector.memset(score_scales[:].bitcast(I32), 0)
+        nc.gpsimd.memset(w_scale_in[:].bitcast(I32), 0)
+
+        nc.sync.dma_start(kidx_sb[:], kidx)
+        nc.scalar.dma_start(d_scale_table[:].bitcast(I32)[0:P:8, :], d_scales[0].bitcast(I32))
+        nc.sync.dma_start(offs_sb[:], offs)
+        nc.scalar.dma_start(x_scale_table[:].bitcast(I32)[0:P:8, :], x_scales[0].bitcast(I32))
+        nc.sync.dma_start(kb_sb[:], kb.rearrange("(p t) o -> p (t o)", t=PACK))
+        nc.sync.dma_start(gn_sb[:], gn.rearrange("(p t) o -> p (t o)", t=PACK))
+        nc.sync.dma_start(d_word_table[:].bitcast(I32), d_words[0].rearrange("p n t -> p (n t)").bitcast(I32))
+        nc.sync.dma_start(x_word_table[:].bitcast(I32), x_words[0].rearrange("p n t -> p (n t)").bitcast(I32))
+        nc.sync.dma_start(w_word_in[:].bitcast(I32), w1_words[0].rearrange("p n t -> p (n t)").bitcast(I32))
+        for q in range(4):
+            nc.gpsimd.dma_start(w_scale_in[:].bitcast(I32)[32 * q : 32 * q + 4, :], w1_scales[0].bitcast(I32)[4 * q : 4 * q + 4, :])
+
+        d_scale_picked = tile("d_scale_picked", [P, PICKED], U8, tag="d_picked")
+        x_scale_picked = tile("x_scale_picked", [P, PICKED], U8, tag="x_picked")
+        staged_scales = tile("staged_scales", [P, 2 * PICKED], U8)
+        nc.vector.tensor_copy(d_scale_picked[:], d_scale_table[:].indirect(kidx_sb[:]))
+        nc.vector.tensor_copy(x_scale_picked[:], x_scale_table[:].indirect(offs_sb[:]))
+        deal(nc, staged_scales[:, :PICKED], d_scale_picked[:], 16)
+        nc.vector.tensor_copy(staged_scales[:, PICKED:].bitcast(I32), x_scale_picked[:].bitcast(I32))
+        for r in range(4):
+            nc.scalar.dma_start(score_scales[:].bitcast(I32)[r:P:32, :], staged_scales[:].bitcast(I32)[8 * r : P : 32, :])
+        key_scales = score_scales[:, :PICKED]
+        query_scales = score_scales[:, PICKED:]
+
+        d_word_picked = tile("d_word_picked", [P, PICKED], U32, tag="d_picked")
+        key_words = tile("key_words", [P, PICKED], U32)
+        nc.vector.tensor_copy(d_word_picked[:], d_word_table[:].indirect(kidx_sb[:]))
+        deal(nc, key_words[:].bitcast(I32), d_word_picked[:].bitcast(I32), 4)
+
+        tanh_tiles = []
+        for h in range(PICKED // HALF):
+            query_words = tile("query_words%d" % h, [P, HALF], U32)
+            nc.vector.tensor_copy(query_words[:], x_word_table[:].indirect(offs_sb[:, h * HALF // 16 : (h + 1) * HALF // 16]))
+            th = tile("tanh%d" % h, [P, PACK, HALF], F32)
+            tanh_tiles.append(th)
+            for pair in range(2):
+                scores = ps.tile([P, 2, HALF], F32, name="scores%d_%d" % (h, pair))
+                for u in range(2):
+                    t = 2 * pair + u
+                    nc.tensor.matmul_mx(
+                        out=scores[:, u, :],
+                        lhsT=key_words[:, t * P : (t + 1) * P].bitcast(FP8X4),
+                        lhsT_scale=key_scales[:, t * P : (t + 1) * P],
+                        rhs=query_words[:].bitcast(FP8X4),
+                        rhs_scale=query_scales[:, h * HALF : (h + 1) * HALF],
+                        start=True,
+                        stop=True,
+                    )
+                for u in range(2):
+                    t = 2 * pair + u
+                    nc.scalar.activation(out=th[:, t, :], in_=scores[:, u, :], func=ACT.Tanh, bias=kb_sb[:, t : t + 1], scale=0.0625)
+
+        value_words = tile("value_words", [P, PICKED], U32, tag="d_picked")
+        value_scales = tile("value_scales", [P, PICKED], U8, tag="x_picked")
+        deal(nc, value_words[:].bitcast(I32), w_word_in[:].bitcast(I32), 4)
+        deal(nc, value_scales[:], w_scale_in[:], 16)
+
+        out_rows = out_0.rearrange("(p t) j -> p t j", t=PACK)
+        out_words_hbm = out_1[0].rearrange("p n t -> p (n t)").bitcast(I32)
+        out_scales = tile("out_scales", [P, PICKED], U8)
+
+        def weigh(c):
+            th = tanh_tiles[c // 2]
+            j0 = (c % 2) * QUARTER
+            z = tile("z%d" % c, [P, QUARTER * PACK], BF16)
+            nc.vector.tensor_tensor(
+                out=z[:].rearrange("p (c i t) -> p c t i", t=PACK, i=4),
+                in0=th[:, :, j0 : j0 + QUARTER].rearrange("p t (c i) -> p c t i", i=4),
+                in1=gn_sb[:].unsqueeze(1).unsqueeze(3).to_broadcast([P, QUARTER // 4, PACK, 4]),
+                op=ALU.mult,
+            )
+            return z
+
+        def second(c, z):
+            z_words = tile("z_words%d" % c, [P, QUARTER], U32)
+            z_scales = tile("z_scales%d" % c, [P, QUARTER], U8)
+            nc.vector.quantize_mx(out=z_words[:].bitcast(FP8X4), scales=z_scales[:], in_=z[:])
+            acc = ps.tile([P, PACK, QUARTER], F32, name="acc%d" % c)
+            for t in range(PACK):
+                nc.tensor.matmul_mx(
+                    out=acc[:, t, :],
+                    lhsT=value_words[:, t * P : (t + 1) * P].bitcast(FP8X4),
+                    lhsT_scale=value_scales[:, t * P : (t + 1) * P],
+                    rhs=z_words[:].bitcast(FP8X4),
+                    rhs_scale=z_scales[:],
+                    start=True,
+                    stop=True,
+                )
+            y = tile("y%d" % c, [P, PACK, QUARTER], F32)
+            nc.scalar.copy(out=y[:], in_=acc[:])
+            nc.sync.dma_start(out_rows[:, :, c * QUARTER : (c + 1) * QUARTER], y[:])
+            return y
+
+        def planes(c, y):
+            yb = tile("yb%d" % c, [P, QUARTER * PACK], BF16)
+            nc.vector.tensor_copy(
+                out=yb[:].rearrange("p (c i t) -> p c t i", t=PACK, i=4),
+                in_=y[:].rearrange("p t (c i) -> p c t i", i=4),
+            )
+            y_words = tile("y_words%d" % c, [P, QUARTER], U32)
+            nc.vector.quantize_mx(out=y_words[:].bitcast(FP8X4), scales=out_scales[:, c * QUARTER : (c + 1) * QUARTER], in_=yb[:])
+            nc.sync.dma_start(out_words_hbm[:, c * QUARTER : (c + 1) * QUARTER], y_words[:].bitcast(I32))
+
+        n = PICKED // QUARTER
+        zs = {}
+        ys = {}
+        for step in range(n + 3):
+            if step < n:
+                zs[step] = weigh(step)
+            if 0 <= step - 1 < n:
+                ys[step - 1] = second(step - 1, zs[step - 1])
+            if 0 <= step - 3 < n:
+                planes(step - 3, ys[step - 3])
+        for q in range(4):
+            eng = nc.sync if q % 2 == 0 else nc.scalar
+            eng.dma_start(out_2[0].bitcast(I32)[4 * q : 4 * q + 4, :], out_scales[:].bitcast(I32)[32 * q : 32 * q + 4, :])

@@ -17,7 +17,7 @@ PACK = 4
 TABLE = 2048
 PICKED = 512
 HALF = 256
-QUARTER = 128
+CHUNKS = (128, 128, 128, 64, 64)
 FLOPS = 2 * 2 * 512 * 512 * 512
 
 
@@ -46,94 +46,101 @@ def tile_picked_sigattn_tanh_po_kernel(
         d_word_table = tile("d_word_table", [P, TABLE], U32)
         x_word_table = tile("x_word_table", [P, TABLE], U32)
         w_word_in = tile("w_word_in", [P, PICKED], U32)
-        w_scale_in = tile("w_scale_in", [P, PICKED], U8)
-        score_scales = tile("score_scales", [P, 2 * PICKED], U8)
+        mx_scales = tile("mx_scales", [P, 3 * PICKED], U8)
         kb_sb = tile("kb_sb", [P, PACK], F32)
         gn_sb = tile("gn_sb", [P, PACK], F32)
 
+        staged_scales = tile("staged_scales", [P, 3 * PICKED], U8)
         nc.vector.memset(d_scale_table[:].bitcast(I32), 0)
         nc.vector.memset(x_scale_table[:].bitcast(I32), 0)
-        nc.vector.memset(score_scales[:].bitcast(I32), 0)
-        nc.gpsimd.memset(w_scale_in[:].bitcast(I32), 0)
+        nc.vector.memset(mx_scales[:].bitcast(I32), 0)
 
         nc.sync.dma_start(kidx_sb[:], kidx)
         nc.scalar.dma_start(d_scale_table[:].bitcast(I32)[0:P:8, :], d_scales[0].bitcast(I32))
         nc.sync.dma_start(offs_sb[:], offs)
         nc.scalar.dma_start(x_scale_table[:].bitcast(I32)[0:P:8, :], x_scales[0].bitcast(I32))
-        nc.sync.dma_start(kb_sb[:], kb.rearrange("(p t) o -> p (t o)", t=PACK))
-        nc.sync.dma_start(gn_sb[:], gn.rearrange("(p t) o -> p (t o)", t=PACK))
+        nc.sync.dma_start(staged_scales[:, 2 * PICKED :].bitcast(I32)[0:P:8, :], w1_scales[0].bitcast(I32))
         nc.sync.dma_start(d_word_table[:].bitcast(I32), d_words[0].rearrange("p n t -> p (n t)").bitcast(I32))
         nc.sync.dma_start(x_word_table[:].bitcast(I32), x_words[0].rearrange("p n t -> p (n t)").bitcast(I32))
         nc.sync.dma_start(w_word_in[:].bitcast(I32), w1_words[0].rearrange("p n t -> p (n t)").bitcast(I32))
-        for q in range(4):
-            nc.gpsimd.dma_start(w_scale_in[:].bitcast(I32)[32 * q : 32 * q + 4, :], w1_scales[0].bitcast(I32)[4 * q : 4 * q + 4, :])
+        nc.gpsimd.dma_start(kb_sb[:], kb.rearrange("(p t) o -> p (t o)", t=PACK))
+        nc.gpsimd.dma_start(gn_sb[:], gn.rearrange("(p t) o -> p (t o)", t=PACK))
 
         d_scale_picked = tile("d_scale_picked", [P, PICKED], U8, tag="d_picked")
         x_scale_picked = tile("x_scale_picked", [P, PICKED], U8, tag="x_picked")
-        staged_scales = tile("staged_scales", [P, 2 * PICKED], U8)
         nc.vector.tensor_copy(d_scale_picked[:], d_scale_table[:].indirect(kidx_sb[:]))
         nc.vector.tensor_copy(x_scale_picked[:], x_scale_table[:].indirect(offs_sb[:]))
         deal(nc, staged_scales[:, :PICKED], d_scale_picked[:], 16)
-        nc.vector.tensor_copy(staged_scales[:, PICKED:].bitcast(I32), x_scale_picked[:].bitcast(I32))
+        nc.vector.tensor_copy(staged_scales[:, PICKED : 2 * PICKED].bitcast(I32), x_scale_picked[:].bitcast(I32))
         for r in range(4):
-            nc.scalar.dma_start(score_scales[:].bitcast(I32)[r:P:32, :], staged_scales[:].bitcast(I32)[8 * r : P : 32, :])
-        key_scales = score_scales[:, :PICKED]
-        query_scales = score_scales[:, PICKED:]
+            nc.scalar.dma_start(mx_scales[:].bitcast(I32)[r:P:32, :], staged_scales[:].bitcast(I32)[8 * r : P : 32, :])
+        key_scales = mx_scales[:, :PICKED]
+        query_scales = mx_scales[:, PICKED : 2 * PICKED]
 
         d_word_picked = tile("d_word_picked", [P, PICKED], U32, tag="d_picked")
         key_words = tile("key_words", [P, PICKED], U32)
         nc.vector.tensor_copy(d_word_picked[:], d_word_table[:].indirect(kidx_sb[:]))
         deal(nc, key_words[:].bitcast(I32), d_word_picked[:].bitcast(I32), 4)
 
-        tanh_tiles = []
+        def score(bank, t, query_words, j0, width):
+            nc.tensor.matmul_mx(
+                out=bank,
+                lhsT=key_words[:, t * P : (t + 1) * P].bitcast(FP8X4),
+                lhsT_scale=key_scales[:, t * P : (t + 1) * P],
+                rhs=query_words[:, j0 % HALF : j0 % HALF + width].bitcast(FP8X4),
+                rhs_scale=query_scales[:, j0 : j0 + width],
+                start=True,
+                stop=True,
+            )
+
+        query_halves = []
         for h in range(PICKED // HALF):
-            query_words = tile("query_words%d" % h, [P, HALF], U32)
+            query_words = tile("query_words%d" % h, [P, HALF], U32, tag="x_picked" if h == 0 else None)
             nc.vector.tensor_copy(query_words[:], x_word_table[:].indirect(offs_sb[:, h * HALF // 16 : (h + 1) * HALF // 16]))
-            th = tile("tanh%d" % h, [P, PACK, HALF], F32)
+            query_halves.append(query_words)
+
+        chunks = []
+        for width in CHUNKS:
+            chunks.append((sum(w for j, w in chunks), width))
+
+        tanh_tiles = []
+        for j0, width in chunks:
+            th = tile("tanh%d" % j0, [P, PACK, width], F32)
+            scores = ps.tile([P, PACK, width], F32, name="scores", bufs=4)
+            for t in range(PACK):
+                score(scores[:, t, :], t, query_halves[j0 // HALF], j0, width)
+            for t in range(PACK):
+                nc.scalar.activation(out=th[:, t, :], in_=scores[:, t, :], func=ACT.Tanh, bias=kb_sb[:, t : t + 1], scale=0.0625)
             tanh_tiles.append(th)
-            for pair in range(2):
-                scores = ps.tile([P, 2, HALF], F32, name="scores%d_%d" % (h, pair))
-                for u in range(2):
-                    t = 2 * pair + u
-                    nc.tensor.matmul_mx(
-                        out=scores[:, u, :],
-                        lhsT=key_words[:, t * P : (t + 1) * P].bitcast(FP8X4),
-                        lhsT_scale=key_scales[:, t * P : (t + 1) * P],
-                        rhs=query_words[:].bitcast(FP8X4),
-                        rhs_scale=query_scales[:, h * HALF : (h + 1) * HALF],
-                        start=True,
-                        stop=True,
-                    )
-                for u in range(2):
-                    t = 2 * pair + u
-                    nc.scalar.activation(out=th[:, t, :], in_=scores[:, u, :], func=ACT.Tanh, bias=kb_sb[:, t : t + 1], scale=0.0625)
 
         value_words = tile("value_words", [P, PICKED], U32, tag="d_picked")
-        value_scales = tile("value_scales", [P, PICKED], U8, tag="x_picked")
+        value_scales = tile("value_scales", [P, PICKED], U8)
         deal(nc, value_words[:].bitcast(I32), w_word_in[:].bitcast(I32), 4)
-        deal(nc, value_scales[:], w_scale_in[:], 16)
+        deal(nc, value_scales[:], mx_scales[:, 2 * PICKED :], 16)
 
         out_rows = out_0.rearrange("(p t) j -> p t j", t=PACK)
         out_words_hbm = out_1[0].rearrange("p n t -> p (n t)").bitcast(I32)
         out_scales = tile("out_scales", [P, PICKED], U8)
 
+        out_words = tile("out_words", [P, PICKED], U32)
+
         def weigh(c):
-            th = tanh_tiles[c // 2]
-            j0 = (c % 2) * QUARTER
-            z = tile("z%d" % c, [P, QUARTER * PACK], BF16)
+            j0, width = chunks[c]
+            z = tile("z%d" % c, [P, width * PACK], BF16)
             nc.vector.tensor_tensor(
                 out=z[:].rearrange("p (c i t) -> p c t i", t=PACK, i=4),
-                in0=th[:, :, j0 : j0 + QUARTER].rearrange("p t (c i) -> p c t i", i=4),
-                in1=gn_sb[:].unsqueeze(1).unsqueeze(3).to_broadcast([P, QUARTER // 4, PACK, 4]),
+                in0=tanh_tiles[c][:].rearrange("p t (c i) -> p c t i", i=4),
+                in1=gn_sb[:].unsqueeze(1).unsqueeze(3).to_broadcast([P, width // 4, PACK, 4]),
                 op=ALU.mult,
             )
             return z
 
         def second(c, z):
-            z_words = tile("z_words%d" % c, [P, QUARTER], U32)
-            z_scales = tile("z_scales%d" % c, [P, QUARTER], U8)
+            j0, width = chunks[c]
+            z_words = tile("z_words%d" % c, [P, width], U32)
+            z_scales = tile("z_scales%d" % c, [P, width], U8)
             nc.vector.quantize_mx(out=z_words[:].bitcast(FP8X4), scales=z_scales[:], in_=z[:])
-            acc = ps.tile([P, PACK, QUARTER], F32, name="acc%d" % c)
+            acc = ps.tile([P, PACK, width], F32, name="acc", bufs=4)
             for t in range(PACK):
                 nc.tensor.matmul_mx(
                     out=acc[:, t, :],
@@ -144,31 +151,27 @@ def tile_picked_sigattn_tanh_po_kernel(
                     start=True,
                     stop=True,
                 )
-            y = tile("y%d" % c, [P, PACK, QUARTER], F32)
+            y = tile("y%d" % c, [P, PACK, width], F32)
             nc.scalar.copy(out=y[:], in_=acc[:])
-            nc.sync.dma_start(out_rows[:, :, c * QUARTER : (c + 1) * QUARTER], y[:])
+            nc.sync.dma_start(out_rows[:, :, j0 : j0 + width], y[:])
             return y
 
         def planes(c, y):
-            yb = tile("yb%d" % c, [P, QUARTER * PACK], BF16)
+            j0, width = chunks[c]
+            yb = tile("yb%d" % c, [P, width * PACK], BF16)
             nc.vector.tensor_copy(
                 out=yb[:].rearrange("p (c i t) -> p c t i", t=PACK, i=4),
                 in_=y[:].rearrange("p t (c i) -> p c t i", i=4),
             )
-            y_words = tile("y_words%d" % c, [P, QUARTER], U32)
-            nc.vector.quantize_mx(out=y_words[:].bitcast(FP8X4), scales=out_scales[:, c * QUARTER : (c + 1) * QUARTER], in_=yb[:])
-            nc.sync.dma_start(out_words_hbm[:, c * QUARTER : (c + 1) * QUARTER], y_words[:].bitcast(I32))
+            nc.vector.quantize_mx(out=out_words[:, j0 : j0 + width].bitcast(FP8X4), scales=out_scales[:, j0 : j0 + width], in_=yb[:])
+            if j0 + width in (HALF, PICKED):
+                cols = slice(j0 + width - HALF, j0 + width)
+                nc.sync.dma_start(out_words_hbm[:, cols], out_words[:, cols].bitcast(I32))
 
-        n = PICKED // QUARTER
-        zs = {}
-        ys = {}
-        for step in range(n + 3):
-            if step < n:
-                zs[step] = weigh(step)
-            if 0 <= step - 1 < n:
-                ys[step - 1] = second(step - 1, zs[step - 1])
-            if 0 <= step - 3 < n:
-                planes(step - 3, ys[step - 3])
+        n = len(chunks)
+        ys = [second(c, weigh(c)) for c in range(n)]
+        for c in range(n):
+            planes(c, ys[c])
         for q in range(4):
-            eng = nc.sync if q % 2 == 0 else nc.scalar
+            eng = nc.scalar if q % 2 == 0 else nc.sync
             eng.dma_start(out_2[0].bitcast(I32)[4 * q : 4 * q + 4, :], out_scales[:].bitcast(I32)[32 * q : 32 * q + 4, :])

@@ -52,19 +52,19 @@ def tile_picked_sigattn_tanh_po_kernel(
 
         staged_scales = tile("staged_scales", [P, 3 * PICKED], U8)
         nc.vector.memset(d_scale_table[:].bitcast(I32), 0)
-        nc.vector.memset(x_scale_table[:].bitcast(I32), 0)
+        nc.gpsimd.memset(x_scale_table[:].bitcast(I32), 0)
         nc.vector.memset(mx_scales[:].bitcast(I32), 0)
 
         nc.sync.dma_start(kidx_sb[:], kidx)
-        nc.scalar.dma_start(d_scale_table[:].bitcast(I32)[0:P:8, :], d_scales[0].bitcast(I32))
         nc.sync.dma_start(offs_sb[:], offs)
+        nc.scalar.dma_start(kb_sb[:], kb.rearrange("(p t) o -> p (t o)", t=PACK))
+        nc.scalar.dma_start(gn_sb[:], gn.rearrange("(p t) o -> p (t o)", t=PACK))
+        nc.scalar.dma_start(staged_scales[:, 2 * PICKED :].bitcast(I32)[0:P:8, :], w1_scales[0].bitcast(I32))
+        nc.scalar.dma_start(d_scale_table[:].bitcast(I32)[0:P:8, :], d_scales[0].bitcast(I32))
         nc.scalar.dma_start(x_scale_table[:].bitcast(I32)[0:P:8, :], x_scales[0].bitcast(I32))
-        nc.sync.dma_start(staged_scales[:, 2 * PICKED :].bitcast(I32)[0:P:8, :], w1_scales[0].bitcast(I32))
-        nc.sync.dma_start(d_word_table[:].bitcast(I32), d_words[0].rearrange("p n t -> p (n t)").bitcast(I32))
-        nc.sync.dma_start(x_word_table[:].bitcast(I32), x_words[0].rearrange("p n t -> p (n t)").bitcast(I32))
-        nc.sync.dma_start(w_word_in[:].bitcast(I32), w1_words[0].rearrange("p n t -> p (n t)").bitcast(I32))
-        nc.gpsimd.dma_start(kb_sb[:], kb.rearrange("(p t) o -> p (t o)", t=PACK))
-        nc.gpsimd.dma_start(gn_sb[:], gn.rearrange("(p t) o -> p (t o)", t=PACK))
+        nc.scalar.dma_start(d_word_table[:].bitcast(I32), d_words[0].rearrange("p n t -> p (n t)").bitcast(I32))
+        nc.scalar.dma_start(x_word_table[:].bitcast(I32), x_words[0].rearrange("p n t -> p (n t)").bitcast(I32))
+        nc.scalar.dma_start(w_word_in[:].bitcast(I32), w1_words[0].rearrange("p n t -> p (n t)").bitcast(I32))
 
         d_scale_picked = tile("d_scale_picked", [P, PICKED], U8, tag="d_picked")
         x_scale_picked = tile("x_scale_picked", [P, PICKED], U8, tag="x_picked")
@@ -73,7 +73,7 @@ def tile_picked_sigattn_tanh_po_kernel(
         deal(nc, staged_scales[:, :PICKED], d_scale_picked[:], 16)
         nc.vector.tensor_copy(staged_scales[:, PICKED : 2 * PICKED].bitcast(I32), x_scale_picked[:].bitcast(I32))
         for r in range(4):
-            nc.scalar.dma_start(mx_scales[:].bitcast(I32)[r:P:32, :], staged_scales[:].bitcast(I32)[8 * r : P : 32, :])
+            nc.sync.dma_start(mx_scales[:].bitcast(I32)[r:P:32, :], staged_scales[:].bitcast(I32)[8 * r : P : 32, :])
         key_scales = mx_scales[:, :PICKED]
         query_scales = mx_scales[:, PICKED : 2 * PICKED]
 

@@ -18,6 +18,7 @@ TABLE = 2048
 PICKED = 512
 HALF = 256
 CHUNKS = (128, 128, 128, 64, 64)
+LAG = 2
 FLOPS = 2 * 2 * 512 * 512 * 512
 
 
@@ -45,7 +46,6 @@ def tile_picked_sigattn_tanh_po_kernel(
         x_scale_table = tile("x_scale_table", [P, TABLE], U8)
         d_word_table = tile("d_word_table", [P, TABLE], U32)
         x_word_table = tile("x_word_table", [P, TABLE], U32)
-        w_word_in = tile("w_word_in", [P, PICKED], U32)
         mx_scales = tile("mx_scales", [P, 3 * PICKED], U8)
         kb_sb = tile("kb_sb", [P, PACK], F32)
         gn_sb = tile("gn_sb", [P, PACK], F32)
@@ -64,7 +64,6 @@ def tile_picked_sigattn_tanh_po_kernel(
         nc.scalar.dma_start(x_scale_table[:].bitcast(I32)[0:P:8, :], x_scales[0].bitcast(I32))
         nc.scalar.dma_start(d_word_table[:].bitcast(I32), d_words[0].rearrange("p n t -> p (n t)").bitcast(I32))
         nc.scalar.dma_start(x_word_table[:].bitcast(I32), x_words[0].rearrange("p n t -> p (n t)").bitcast(I32))
-        nc.scalar.dma_start(w_word_in[:].bitcast(I32), w1_words[0].rearrange("p n t -> p (n t)").bitcast(I32))
 
         d_scale_picked = tile("d_scale_picked", [P, PICKED], U8, tag="d_picked")
         x_scale_picked = tile("x_scale_picked", [P, PICKED], U8, tag="x_picked")
@@ -74,6 +73,8 @@ def tile_picked_sigattn_tanh_po_kernel(
         nc.vector.tensor_copy(staged_scales[:, PICKED : 2 * PICKED].bitcast(I32), x_scale_picked[:].bitcast(I32))
         for r in range(4):
             nc.sync.dma_start(mx_scales[:].bitcast(I32)[r:P:32, :], staged_scales[:].bitcast(I32)[8 * r : P : 32, :])
+        w_word_in = tile("w_word_in", [P, PICKED], U32, tag="x_picked")
+        nc.sync.dma_start(w_word_in[:].bitcast(I32), w1_words[0].rearrange("p n t -> p (n t)").bitcast(I32))
         key_scales = mx_scales[:, :PICKED]
         query_scales = mx_scales[:, PICKED : 2 * PICKED]
 
@@ -95,7 +96,7 @@ def tile_picked_sigattn_tanh_po_kernel(
 
         query_halves = []
         for h in range(PICKED // HALF):
-            query_words = tile("query_words%d" % h, [P, HALF], U32, tag="x_picked" if h == 0 else None)
+            query_words = tile("query_words%d" % h, [P, HALF], U32)
             nc.vector.tensor_copy(query_words[:], x_word_table[:].indirect(offs_sb[:, h * HALF // 16 : (h + 1) * HALF // 16]))
             query_halves.append(query_words)
 
@@ -103,15 +104,15 @@ def tile_picked_sigattn_tanh_po_kernel(
         for width in CHUNKS:
             chunks.append((sum(w for j, w in chunks), width))
 
-        tanh_tiles = []
-        for j0, width in chunks:
+        def first(c):
+            j0, width = chunks[c]
             th = tile("tanh%d" % j0, [P, PACK, width], F32)
             scores = ps.tile([P, PACK, width], F32, name="scores", bufs=4)
             for t in range(PACK):
                 score(scores[:, t, :], t, query_halves[j0 // HALF], j0, width)
             for t in range(PACK):
                 nc.scalar.activation(out=th[:, t, :], in_=scores[:, t, :], func=ACT.Tanh, bias=kb_sb[:, t : t + 1], scale=0.0625)
-            tanh_tiles.append(th)
+            return th
 
         value_words = tile("value_words", [P, PICKED], U32, tag="d_picked")
         value_scales = tile("value_scales", [P, PICKED], U8)
@@ -124,12 +125,12 @@ def tile_picked_sigattn_tanh_po_kernel(
 
         out_words = tile("out_words", [P, PICKED], U32)
 
-        def weigh(c):
+        def weigh(c, th):
             j0, width = chunks[c]
             z = tile("z%d" % c, [P, width * PACK], BF16)
             nc.vector.tensor_tensor(
                 out=z[:].rearrange("p (c i t) -> p c t i", t=PACK, i=4),
-                in0=tanh_tiles[c][:].rearrange("p t (c i) -> p c t i", i=4),
+                in0=th[:].rearrange("p t (c i) -> p c t i", i=4),
                 in1=gn_sb[:].unsqueeze(1).unsqueeze(3).to_broadcast([P, width // 4, PACK, 4]),
                 op=ALU.mult,
             )
@@ -169,7 +170,13 @@ def tile_picked_sigattn_tanh_po_kernel(
                 nc.sync.dma_start(out_words_hbm[:, cols], out_words[:, cols].bitcast(I32))
 
         n = len(chunks)
-        ys = [second(c, weigh(c)) for c in range(n)]
+        ths = []
+        ys = []
+        for step in range(n + LAG):
+            if step < n:
+                ths.append(first(step))
+            if step >= LAG:
+                ys.append(second(step - LAG, weigh(step - LAG, ths[step - LAG])))
         for c in range(n):
             planes(c, ys[c])
         for q in range(4):

@@ -46,39 +46,41 @@ def tile_picked_sigattn_tanh_po_kernel(
         x_scale_table = tile("x_scale_table", [P, TABLE], U8)
         d_word_table = tile("d_word_table", [P, TABLE], U32)
         x_word_table = tile("x_word_table", [P, TABLE], U32)
-        mx_scales = tile("mx_scales", [P, 3 * PICKED], U8)
+        mx_scales = tile("mx_scales", [P, 2 * PICKED], U8)
         kb_sb = tile("kb_sb", [P, PACK], F32)
         gn_sb = tile("gn_sb", [P, PACK], F32)
-
-        staged_scales = tile("staged_scales", [P, 3 * PICKED], U8)
+        w_scale_in = tile("w_scale_in", [P, PICKED], U8)
+        w_word_in = tile("w_word_in", [P, PICKED], U32)
         nc.vector.memset(d_scale_table[:].bitcast(I32), 0)
-        nc.gpsimd.memset(x_scale_table[:].bitcast(I32), 0)
-        nc.vector.memset(mx_scales[:].bitcast(I32), 0)
+        nc.gpsimd.memset(w_scale_in[:].bitcast(I32), 0)
+        nc.vector.memset(x_scale_table[:, : TABLE // 2].bitcast(I32), 0)
+        nc.gpsimd.memset(x_scale_table[:, TABLE // 2 :].bitcast(I32), 0)
 
         nc.sync.dma_start(kidx_sb[:], kidx)
-        nc.sync.dma_start(offs_sb[:], offs)
-        nc.scalar.dma_start(kb_sb[:], kb.rearrange("(p t) o -> p (t o)", t=PACK))
-        nc.scalar.dma_start(gn_sb[:], gn.rearrange("(p t) o -> p (t o)", t=PACK))
-        nc.scalar.dma_start(staged_scales[:, 2 * PICKED :].bitcast(I32)[0:P:8, :], w1_scales[0].bitcast(I32))
-        nc.scalar.dma_start(d_scale_table[:].bitcast(I32)[0:P:8, :], d_scales[0].bitcast(I32))
-        nc.scalar.dma_start(x_scale_table[:].bitcast(I32)[0:P:8, :], x_scales[0].bitcast(I32))
-        nc.scalar.dma_start(d_word_table[:].bitcast(I32), d_words[0].rearrange("p n t -> p (n t)").bitcast(I32))
-        nc.scalar.dma_start(x_word_table[:].bitcast(I32), x_words[0].rearrange("p n t -> p (n t)").bitcast(I32))
-
-        d_scale_picked = tile("d_scale_picked", [P, PICKED], U8, tag="d_picked")
-        x_scale_picked = tile("x_scale_picked", [P, PICKED], U8, tag="x_picked")
-        nc.vector.tensor_copy(d_scale_picked[:], d_scale_table[:].indirect(kidx_sb[:]))
-        nc.vector.tensor_copy(x_scale_picked[:], x_scale_table[:].indirect(offs_sb[:]))
-        deal(nc, staged_scales[:, :PICKED], d_scale_picked[:], 16)
-        nc.vector.tensor_copy(staged_scales[:, PICKED : 2 * PICKED].bitcast(I32), x_scale_picked[:].bitcast(I32))
-        for r in range(4):
-            nc.sync.dma_start(mx_scales[:].bitcast(I32)[r:P:32, :], staged_scales[:].bitcast(I32)[8 * r : P : 32, :])
-        w_word_in = tile("w_word_in", [P, PICKED], U32, tag="x_picked")
         nc.sync.dma_start(w_word_in[:].bitcast(I32), w1_words[0].rearrange("p n t -> p (n t)").bitcast(I32))
-        key_scales = mx_scales[:, :PICKED]
-        query_scales = mx_scales[:, PICKED : 2 * PICKED]
+        nc.sync.dma_start(offs_sb[:], offs)
+        nc.sync.dma_start(w_scale_in[:].bitcast(I32)[0:P:8, :], w1_scales[0].bitcast(I32))
+        nc.scalar.dma_start(kb_sb[:], kb.rearrange("(p t) o -> p (t o)", t=PACK))
+        nc.sync.dma_start(d_scale_table[:].bitcast(I32)[0:P:8, :], d_scales[0].bitcast(I32))
+        nc.sync.dma_start(d_word_table[:].bitcast(I32), d_words[0].rearrange("p n t -> p (n t)").bitcast(I32))
+        for q in range(4):
+            nc.sync.dma_start(x_scale_table[:].bitcast(I32)[32 * q : 32 * q + 4, :], x_scales[0].bitcast(I32)[4 * q : 4 * q + 4, :])
+        nc.sync.dma_start(x_word_table[:].bitcast(I32), x_words[0].rearrange("p n t -> p (n t)").bitcast(I32))
+        nc.scalar.dma_start(gn_sb[:], gn.rearrange("(p t) o -> p (t o)", t=PACK))
 
-        d_word_picked = tile("d_word_picked", [P, PICKED], U32, tag="d_picked")
+        value_words = tile("value_words", [P, PICKED], U32)
+        deal(nc, value_words[:].bitcast(I32), w_word_in[:].bitcast(I32), 4)
+        deal(nc, mx_scales[:, PICKED:], w_scale_in[:], 16)
+        d_scale_picked = tile("d_scale_picked", [P, PICKED], U8)
+        nc.vector.tensor_copy(d_scale_picked[:], d_scale_table[:].indirect(kidx_sb[:]))
+        deal(nc, mx_scales[:, :PICKED], d_scale_picked[:], 16)
+        for r in range(1, 4):
+            eng = nc.sync if r == 2 else nc.scalar
+            eng.dma_start(mx_scales[:].bitcast(I32)[r:P:32, :], mx_scales[:].bitcast(I32)[8 * r : P : 32, :])
+        key_scales = mx_scales[:, :PICKED]
+        value_scales = mx_scales[:, PICKED:]
+
+        d_word_picked = tile("d_word_picked", [P, PICKED], U32)
         key_words = tile("key_words", [P, PICKED], U32)
         nc.vector.tensor_copy(d_word_picked[:], d_word_table[:].indirect(kidx_sb[:]))
         deal(nc, key_words[:].bitcast(I32), d_word_picked[:].bitcast(I32), 4)
@@ -89,16 +91,21 @@ def tile_picked_sigattn_tanh_po_kernel(
                 lhsT=key_words[:, t * P : (t + 1) * P].bitcast(FP8X4),
                 lhsT_scale=key_scales[:, t * P : (t + 1) * P],
                 rhs=query_words[:, j0 % HALF : j0 % HALF + width].bitcast(FP8X4),
-                rhs_scale=query_scales[:, j0 : j0 + width],
+                rhs_scale=query_scales[j0 // HALF][:, j0 % HALF : j0 % HALF + width],
                 start=True,
                 stop=True,
             )
 
+        offs_halves = [offs_sb[:, h * HALF // 16 : (h + 1) * HALF // 16] for h in range(2)]
+        query_scales = [tile("query_scales0", [P, HALF], U8)]
+        nc.vector.tensor_copy(query_scales[0][:], x_scale_table[:].indirect(offs_halves[0]))
         query_halves = []
         for h in range(PICKED // HALF):
             query_words = tile("query_words%d" % h, [P, HALF], U32)
-            nc.vector.tensor_copy(query_words[:], x_word_table[:].indirect(offs_sb[:, h * HALF // 16 : (h + 1) * HALF // 16]))
+            nc.vector.tensor_copy(query_words[:], x_word_table[:].indirect(offs_halves[h]))
             query_halves.append(query_words)
+        query_scales.append(tile("query_scales1", [P, HALF], U8, tag="x_word_table"))
+        nc.vector.tensor_copy(query_scales[1][:], x_scale_table[:].indirect(offs_halves[1]))
 
         chunks = []
         for width in CHUNKS:
@@ -113,11 +120,6 @@ def tile_picked_sigattn_tanh_po_kernel(
             for t in range(PACK):
                 nc.scalar.activation(out=th[:, t, :], in_=scores[:, t, :], func=ACT.Tanh, bias=kb_sb[:, t : t + 1], scale=0.0625)
             return th
-
-        value_words = tile("value_words", [P, PICKED], U32, tag="d_picked")
-        value_scales = tile("value_scales", [P, PICKED], U8)
-        deal(nc, value_words[:].bitcast(I32), w_word_in[:].bitcast(I32), 4)
-        deal(nc, value_scales[:], mx_scales[:, 2 * PICKED :], 16)
 
         out_rows = out_0.rearrange("(p t) j -> p t j", t=PACK)
         out_words_hbm = out_1[0].rearrange("p n t -> p (n t)").bitcast(I32)

@@ -18,7 +18,7 @@ TABLE = 2048
 PICKED = 512
 HALF = 256
 CHUNKS = (128, 128, 128, 64, 64)
-LAG = 2
+SCALAR_FROM = 3
 FLOPS = 2 * 2 * 512 * 512 * 512
 
 
@@ -35,6 +35,7 @@ def tile_picked_sigattn_tanh_po_kernel(
     nc = tc.nc
     with ExitStack() as ctx:
         sb = ctx.enter_context(tc.tile_pool(name="sb", bufs=1))
+        reuse = ctx.enter_context(tc.tile_pool(name="reuse", bufs=1))
         ps = ctx.enter_context(tc.psum_pool(name="ps", bufs=1))
 
         def tile(name, shape, dtype, tag=None):
@@ -46,41 +47,41 @@ def tile_picked_sigattn_tanh_po_kernel(
         x_scale_table = tile("x_scale_table", [P, TABLE], U8)
         d_word_table = tile("d_word_table", [P, TABLE], U32)
         x_word_table = tile("x_word_table", [P, TABLE], U32)
-        mx_scales = tile("mx_scales", [P, 2 * PICKED], U8)
+        mx_scales = tile("mx_scales", [P, 3 * PICKED], U8)
         kb_sb = tile("kb_sb", [P, PACK], F32)
         gn_sb = tile("gn_sb", [P, PACK], F32)
-        w_scale_in = tile("w_scale_in", [P, PICKED], U8)
-        w_word_in = tile("w_word_in", [P, PICKED], U32)
-        nc.vector.memset(d_scale_table[:].bitcast(I32), 0)
-        nc.gpsimd.memset(w_scale_in[:].bitcast(I32), 0)
-        nc.vector.memset(x_scale_table[:, : TABLE // 2].bitcast(I32), 0)
-        nc.gpsimd.memset(x_scale_table[:, TABLE // 2 :].bitcast(I32), 0)
+        w_scale_in = mx_scales[:, 2 * PICKED :]
+        for table in (d_scale_table, x_scale_table):
+            nc.vector.memset(table[:, : TABLE // 2].bitcast(I32), 0)
+            nc.gpsimd.memset(table[:, TABLE // 2 :].bitcast(I32), 0)
+        nc.vector.memset(w_scale_in.bitcast(I32), 0)
 
+        d_words_hbm = d_words[0].rearrange("p n t -> p (n t)").bitcast(I32)
         nc.sync.dma_start(kidx_sb[:], kidx)
-        nc.sync.dma_start(w_word_in[:].bitcast(I32), w1_words[0].rearrange("p n t -> p (n t)").bitcast(I32))
+        nc.sync.dma_start(d_word_table[:].bitcast(I32)[:, : TABLE // 2], d_words_hbm[:, : TABLE // 2])
         nc.sync.dma_start(offs_sb[:], offs)
-        nc.sync.dma_start(w_scale_in[:].bitcast(I32)[0:P:8, :], w1_scales[0].bitcast(I32))
-        nc.scalar.dma_start(kb_sb[:], kb.rearrange("(p t) o -> p (t o)", t=PACK))
+        nc.sync.dma_start(kb_sb[:], kb.rearrange("(p t) o -> p (t o)", t=PACK))
         nc.sync.dma_start(d_scale_table[:].bitcast(I32)[0:P:8, :], d_scales[0].bitcast(I32))
-        nc.sync.dma_start(d_word_table[:].bitcast(I32), d_words[0].rearrange("p n t -> p (n t)").bitcast(I32))
-        for q in range(4):
-            nc.sync.dma_start(x_scale_table[:].bitcast(I32)[32 * q : 32 * q + 4, :], x_scales[0].bitcast(I32)[4 * q : 4 * q + 4, :])
+        nc.sync.dma_start(x_scale_table[:].bitcast(I32)[0:P:8, :], x_scales[0].bitcast(I32))
+        nc.sync.dma_start(w_scale_in.bitcast(I32)[0:P:8, :], w1_scales[0].bitcast(I32))
+        nc.sync.dma_start(d_word_table[:].bitcast(I32)[:, TABLE // 2 :], d_words_hbm[:, TABLE // 2 :])
         nc.sync.dma_start(x_word_table[:].bitcast(I32), x_words[0].rearrange("p n t -> p (n t)").bitcast(I32))
-        nc.scalar.dma_start(gn_sb[:], gn.rearrange("(p t) o -> p (t o)", t=PACK))
+        nc.gpsimd.dma_start(gn_sb[:], gn.rearrange("(p t) o -> p (t o)", t=PACK))
 
-        value_words = tile("value_words", [P, PICKED], U32)
-        deal(nc, value_words[:].bitcast(I32), w_word_in[:].bitcast(I32), 4)
-        deal(nc, mx_scales[:, PICKED:], w_scale_in[:], 16)
         d_scale_picked = tile("d_scale_picked", [P, PICKED], U8)
+        x_scale_picked = reuse.tile([P, PICKED], U8, name="x_scale_picked", offset=4 * PICKED - PICKED // 2)
         nc.vector.tensor_copy(d_scale_picked[:], d_scale_table[:].indirect(kidx_sb[:]))
+        nc.vector.tensor_copy(x_scale_picked[:], x_scale_table[:].indirect(offs_sb[:]))
         deal(nc, mx_scales[:, :PICKED], d_scale_picked[:], 16)
+        nc.vector.tensor_copy(mx_scales[:, PICKED : 2 * PICKED].bitcast(I32), x_scale_picked[:].bitcast(I32))
         for r in range(1, 4):
-            eng = nc.sync if r == 2 else nc.scalar
-            eng.dma_start(mx_scales[:].bitcast(I32)[r:P:32, :], mx_scales[:].bitcast(I32)[8 * r : P : 32, :])
+            nc.sync.dma_start(mx_scales[:].bitcast(I32)[r:P:32, :], mx_scales[:].bitcast(I32)[8 * r : P : 32, :])
+        w_word_in = reuse.tile([P, PICKED], U32, name="w_word_in", offset=4 * PICKED)
+        nc.sync.dma_start(w_word_in[:].bitcast(I32), w1_words[0].rearrange("p n t -> p (n t)").bitcast(I32))
         key_scales = mx_scales[:, :PICKED]
-        value_scales = mx_scales[:, PICKED:]
+        query_scales = mx_scales[:, PICKED : 2 * PICKED]
 
-        d_word_picked = tile("d_word_picked", [P, PICKED], U32)
+        d_word_picked = reuse.tile([P, PICKED], U32, name="d_word_picked", offset=0)
         key_words = tile("key_words", [P, PICKED], U32)
         nc.vector.tensor_copy(d_word_picked[:], d_word_table[:].indirect(kidx_sb[:]))
         deal(nc, key_words[:].bitcast(I32), d_word_picked[:].bitcast(I32), 4)
@@ -91,34 +92,36 @@ def tile_picked_sigattn_tanh_po_kernel(
                 lhsT=key_words[:, t * P : (t + 1) * P].bitcast(FP8X4),
                 lhsT_scale=key_scales[:, t * P : (t + 1) * P],
                 rhs=query_words[:, j0 % HALF : j0 % HALF + width].bitcast(FP8X4),
-                rhs_scale=query_scales[j0 // HALF][:, j0 % HALF : j0 % HALF + width],
+                rhs_scale=query_scales[:, j0 : j0 + width],
                 start=True,
                 stop=True,
             )
 
         offs_halves = [offs_sb[:, h * HALF // 16 : (h + 1) * HALF // 16] for h in range(2)]
-        query_scales = [tile("query_scales0", [P, HALF], U8)]
-        nc.vector.tensor_copy(query_scales[0][:], x_scale_table[:].indirect(offs_halves[0]))
         query_halves = []
         for h in range(PICKED // HALF):
             query_words = tile("query_words%d" % h, [P, HALF], U32)
             nc.vector.tensor_copy(query_words[:], x_word_table[:].indirect(offs_halves[h]))
             query_halves.append(query_words)
-        query_scales.append(tile("query_scales1", [P, HALF], U8, tag="x_word_table"))
-        nc.vector.tensor_copy(query_scales[1][:], x_scale_table[:].indirect(offs_halves[1]))
+        value_words = tile("value_words", [P, PICKED], U32)
+        value_scales = tile("value_scales", [P, PICKED], U8)
+        deal(nc, value_scales[:], w_scale_in, 16)
+        deal(nc, value_words[:].bitcast(I32), w_word_in[:].bitcast(I32), 4)
 
         chunks = []
         for width in CHUNKS:
             chunks.append((sum(w for j, w in chunks), width))
 
-        def first(c):
-            j0, width = chunks[c]
+        def first(j0, width, per_bank):
             th = tile("tanh%d" % j0, [P, PACK, width], F32)
-            scores = ps.tile([P, PACK, width], F32, name="scores", bufs=4)
-            for t in range(PACK):
-                score(scores[:, t, :], t, query_halves[j0 // HALF], j0, width)
-            for t in range(PACK):
-                nc.scalar.activation(out=th[:, t, :], in_=scores[:, t, :], func=ACT.Tanh, bias=kb_sb[:, t : t + 1], scale=0.0625)
+            for t0 in range(0, PACK, per_bank):
+                scores = ps.tile([P, per_bank, width], F32, name="scores", bufs=4)
+                for t in range(per_bank):
+                    score(scores[:, t, :], t0 + t, query_halves[j0 // HALF], j0, width)
+                for t in range(per_bank):
+                    nc.scalar.activation(
+                        out=th[:, t0 + t, :], in_=scores[:, t, :], func=ACT.Tanh, bias=kb_sb[:, t0 + t : t0 + t + 1], scale=0.0625
+                    )
             return th
 
         out_rows = out_0.rearrange("(p t) j -> p t j", t=PACK)
@@ -132,7 +135,7 @@ def tile_picked_sigattn_tanh_po_kernel(
             z = tile("z%d" % c, [P, width * PACK], BF16)
             nc.vector.tensor_tensor(
                 out=z[:].rearrange("p (c i t) -> p c t i", t=PACK, i=4),
-                in0=th[:].rearrange("p t (c i) -> p c t i", i=4),
+                in0=th.rearrange("p t (c i) -> p c t i", i=4),
                 in1=gn_sb[:].unsqueeze(1).unsqueeze(3).to_broadcast([P, width // 4, PACK, 4]),
                 op=ALU.mult,
             )
@@ -155,17 +158,20 @@ def tile_picked_sigattn_tanh_po_kernel(
                     stop=True,
                 )
             y = tile("y%d" % c, [P, PACK, width], F32)
+            yb = tile("yb%d" % c, [P, width * PACK], BF16)
+            if c >= SCALAR_FROM:
+                nc.scalar.copy(out=yb[:].rearrange("p (j t) -> p j t", t=PACK), in_=acc[:].rearrange("p t j -> p j t"))
             nc.scalar.copy(out=y[:], in_=acc[:])
             nc.sync.dma_start(out_rows[:, :, j0 : j0 + width], y[:])
-            return y
+            return y, yb
 
-        def planes(c, y):
+        def planes(c, y, yb):
             j0, width = chunks[c]
-            yb = tile("yb%d" % c, [P, width * PACK], BF16)
-            nc.vector.tensor_copy(
-                out=yb[:].rearrange("p (c i t) -> p c t i", t=PACK, i=4),
-                in_=y[:].rearrange("p t (c i) -> p c t i", i=4),
-            )
+            if c < SCALAR_FROM:
+                nc.vector.tensor_copy(
+                    out=yb[:].rearrange("p (c i t) -> p c t i", t=PACK, i=4),
+                    in_=y[:].rearrange("p t (c i) -> p c t i", i=4),
+                )
             nc.vector.quantize_mx(out=out_words[:, j0 : j0 + width].bitcast(FP8X4), scales=out_scales[:, j0 : j0 + width], in_=yb[:])
             if j0 + width in (HALF, PICKED):
                 cols = slice(j0 + width - HALF, j0 + width)
@@ -174,13 +180,20 @@ def tile_picked_sigattn_tanh_po_kernel(
         n = len(chunks)
         ths = []
         ys = []
-        for step in range(n + LAG):
-            if step < n:
-                ths.append(first(step))
-            if step >= LAG:
-                ys.append(second(step - LAG, weigh(step - LAG, ths[step - LAG])))
+        th = first(0, 128, 2)
+        ths.append(th[:])
+        th = first(128, 128, 4)
+        ths.append(th[:])
+        th = first(256, 128, 4)
+        ths.append(th[:])
+        ys.append(second(0, weigh(0, ths[0])))
+        th = first(384, 128, 4)
+        for j0, width in chunks[3:]:
+            ths.append(th[:, :, j0 - 384 : j0 - 384 + width])
+        for c in range(1, n):
+            ys.append(second(c, weigh(c, ths[c])))
         for c in range(n):
-            planes(c, ys[c])
+            planes(c, *ys[c])
         for q in range(4):
             eng = nc.scalar if q % 2 == 0 else nc.sync
             eng.dma_start(out_2[0].bitcast(I32)[4 * q : 4 * q + 4, :], out_scales[:].bitcast(I32)[32 * q : 32 * q + 4, :])

@@ -18,7 +18,6 @@ TABLE = 2048
 PICKED = 512
 HALF = 256
 CHUNKS = (128, 128, 128, 64, 64)
-SCALAR_FROM = 3
 FLOPS = 2 * 2 * 512 * 512 * 512
 
 
@@ -141,6 +140,8 @@ def tile_picked_sigattn_tanh_po_kernel(
             )
             return z
 
+        y_tiles = []
+
         def second(c, z):
             j0, width = chunks[c]
             z_words = tile("z_words%d" % c, [P, width], U32)
@@ -157,25 +158,24 @@ def tile_picked_sigattn_tanh_po_kernel(
                     start=True,
                     stop=True,
                 )
-            y = tile("y%d" % c, [P, PACK, width], F32)
+            if j0 % P == 0:
+                y_tiles.append(tile("y%d" % c, [P, PACK, P], F32))
+            y = y_tiles[-1][:, :, j0 % P : j0 % P + width]
             yb = tile("yb%d" % c, [P, width * PACK], BF16)
-            if c >= SCALAR_FROM:
-                nc.scalar.copy(out=yb[:].rearrange("p (j t) -> p j t", t=PACK), in_=acc[:].rearrange("p t j -> p j t"))
-            nc.scalar.copy(out=y[:], in_=acc[:])
-            nc.sync.dma_start(out_rows[:, :, j0 : j0 + width], y[:])
+            nc.scalar.copy(out=y, in_=acc[:])
+            if (j0 + width) % P == 0:
+                nc.sync.dma_start(out_rows[:, :, j0 + width - P : j0 + width], y_tiles[-1][:])
             return y, yb
 
         def planes(c, y, yb):
             j0, width = chunks[c]
-            if c < SCALAR_FROM:
-                nc.vector.tensor_copy(
-                    out=yb[:].rearrange("p (c i t) -> p c t i", t=PACK, i=4),
-                    in_=y[:].rearrange("p t (c i) -> p c t i", i=4),
-                )
+            nc.vector.tensor_copy(
+                out=yb[:].rearrange("p (c i t) -> p c t i", t=PACK, i=4),
+                in_=y.rearrange("p t (c i) -> p c t i", i=4),
+            )
             nc.vector.quantize_mx(out=out_words[:, j0 : j0 + width].bitcast(FP8X4), scales=out_scales[:, j0 : j0 + width], in_=yb[:])
-            if j0 + width in (HALF, PICKED):
-                cols = slice(j0 + width - HALF, j0 + width)
-                nc.sync.dma_start(out_words_hbm[:, cols], out_words[:, cols].bitcast(I32))
+            if j0 + width == PICKED:
+                nc.sync.dma_start(out_words_hbm, out_words[:].bitcast(I32))
 
         n = len(chunks)
         ths = []

@@ -34,7 +34,6 @@ def tile_picked_sigattn_tanh_po_kernel(
     nc = tc.nc
     with ExitStack() as ctx:
         sb = ctx.enter_context(tc.tile_pool(name="sb", bufs=1))
-        reuse = ctx.enter_context(tc.tile_pool(name="reuse", bufs=1))
         ps = ctx.enter_context(tc.psum_pool(name="ps", bufs=1))
 
         def tile(name, shape, dtype, tag=None):
@@ -49,38 +48,36 @@ def tile_picked_sigattn_tanh_po_kernel(
         mx_scales = tile("mx_scales", [P, 3 * PICKED], U8)
         kb_sb = tile("kb_sb", [P, PACK], F32)
         gn_sb = tile("gn_sb", [P, PACK], F32)
-        w_scale_in = mx_scales[:, 2 * PICKED :]
-        for table in (d_scale_table, x_scale_table):
-            nc.vector.memset(table[:, : TABLE // 2].bitcast(I32), 0)
-            nc.gpsimd.memset(table[:, TABLE // 2 :].bitcast(I32), 0)
-        nc.vector.memset(w_scale_in.bitcast(I32), 0)
 
-        d_words_hbm = d_words[0].rearrange("p n t -> p (n t)").bitcast(I32)
+        staged_scales = tile("staged_scales", [P, 3 * PICKED], U8)
+        nc.vector.memset(d_scale_table[:].bitcast(I32), 0)
+        nc.gpsimd.memset(x_scale_table[:].bitcast(I32), 0)
+        nc.vector.memset(mx_scales[:].bitcast(I32), 0)
+
         nc.sync.dma_start(kidx_sb[:], kidx)
-        nc.sync.dma_start(d_word_table[:].bitcast(I32)[:, : TABLE // 2], d_words_hbm[:, : TABLE // 2])
         nc.sync.dma_start(offs_sb[:], offs)
-        nc.sync.dma_start(kb_sb[:], kb.rearrange("(p t) o -> p (t o)", t=PACK))
-        nc.sync.dma_start(d_scale_table[:].bitcast(I32)[0:P:8, :], d_scales[0].bitcast(I32))
-        nc.sync.dma_start(x_scale_table[:].bitcast(I32)[0:P:8, :], x_scales[0].bitcast(I32))
-        nc.sync.dma_start(w_scale_in.bitcast(I32)[0:P:8, :], w1_scales[0].bitcast(I32))
-        nc.sync.dma_start(d_word_table[:].bitcast(I32)[:, TABLE // 2 :], d_words_hbm[:, TABLE // 2 :])
-        nc.sync.dma_start(x_word_table[:].bitcast(I32), x_words[0].rearrange("p n t -> p (n t)").bitcast(I32))
-        nc.gpsimd.dma_start(gn_sb[:], gn.rearrange("(p t) o -> p (t o)", t=PACK))
+        nc.scalar.dma_start(kb_sb[:], kb.rearrange("(p t) o -> p (t o)", t=PACK))
+        nc.scalar.dma_start(gn_sb[:], gn.rearrange("(p t) o -> p (t o)", t=PACK))
+        nc.scalar.dma_start(staged_scales[:, 2 * PICKED :].bitcast(I32)[0:P:8, :], w1_scales[0].bitcast(I32))
+        nc.scalar.dma_start(d_scale_table[:].bitcast(I32)[0:P:8, :], d_scales[0].bitcast(I32))
+        nc.scalar.dma_start(x_scale_table[:].bitcast(I32)[0:P:8, :], x_scales[0].bitcast(I32))
+        nc.scalar.dma_start(d_word_table[:].bitcast(I32), d_words[0].rearrange("p n t -> p (n t)").bitcast(I32))
+        nc.scalar.dma_start(x_word_table[:].bitcast(I32), x_words[0].rearrange("p n t -> p (n t)").bitcast(I32))
 
-        d_scale_picked = tile("d_scale_picked", [P, PICKED], U8)
-        x_scale_picked = reuse.tile([P, PICKED], U8, name="x_scale_picked", offset=4 * PICKED - PICKED // 2)
+        d_scale_picked = tile("d_scale_picked", [P, PICKED], U8, tag="d_picked")
+        x_scale_picked = tile("x_scale_picked", [P, PICKED], U8, tag="x_picked")
         nc.vector.tensor_copy(d_scale_picked[:], d_scale_table[:].indirect(kidx_sb[:]))
         nc.vector.tensor_copy(x_scale_picked[:], x_scale_table[:].indirect(offs_sb[:]))
-        deal(nc, mx_scales[:, :PICKED], d_scale_picked[:], 16)
-        nc.vector.tensor_copy(mx_scales[:, PICKED : 2 * PICKED].bitcast(I32), x_scale_picked[:].bitcast(I32))
-        for r in range(1, 4):
-            nc.sync.dma_start(mx_scales[:].bitcast(I32)[r:P:32, :], mx_scales[:].bitcast(I32)[8 * r : P : 32, :])
-        w_word_in = reuse.tile([P, PICKED], U32, name="w_word_in", offset=4 * PICKED)
+        deal(nc, staged_scales[:, :PICKED], d_scale_picked[:], 16)
+        nc.vector.tensor_copy(staged_scales[:, PICKED : 2 * PICKED].bitcast(I32), x_scale_picked[:].bitcast(I32))
+        for r in range(4):
+            nc.sync.dma_start(mx_scales[:].bitcast(I32)[r:P:32, :], staged_scales[:].bitcast(I32)[8 * r : P : 32, :])
+        w_word_in = tile("w_word_in", [P, PICKED], U32, tag="x_picked")
         nc.sync.dma_start(w_word_in[:].bitcast(I32), w1_words[0].rearrange("p n t -> p (n t)").bitcast(I32))
         key_scales = mx_scales[:, :PICKED]
         query_scales = mx_scales[:, PICKED : 2 * PICKED]
 
-        d_word_picked = reuse.tile([P, PICKED], U32, name="d_word_picked", offset=0)
+        d_word_picked = tile("d_word_picked", [P, PICKED], U32, tag="d_picked")
         key_words = tile("key_words", [P, PICKED], U32)
         nc.vector.tensor_copy(d_word_picked[:], d_word_table[:].indirect(kidx_sb[:]))
         deal(nc, key_words[:].bitcast(I32), d_word_picked[:].bitcast(I32), 4)
@@ -102,9 +99,9 @@ def tile_picked_sigattn_tanh_po_kernel(
             query_words = tile("query_words%d" % h, [P, HALF], U32)
             nc.vector.tensor_copy(query_words[:], x_word_table[:].indirect(offs_halves[h]))
             query_halves.append(query_words)
-        value_words = tile("value_words", [P, PICKED], U32)
+        value_words = tile("value_words", [P, PICKED], U32, tag="d_picked")
         value_scales = tile("value_scales", [P, PICKED], U8)
-        deal(nc, value_scales[:], w_scale_in, 16)
+        deal(nc, value_scales[:], mx_scales[:, 2 * PICKED :], 16)
         deal(nc, value_words[:].bitcast(I32), w_word_in[:].bitcast(I32), 4)
 
         chunks = []

@@ -81,6 +81,17 @@ def tile_picked_sigattn_tanh_po_kernel(
         key_words = tile("key_words", [P, PICKED], U32)
         nc.vector.tensor_copy(d_word_picked[:], d_word_table[:].indirect(kidx_sb[:]))
         deal(nc, key_words[:].bitcast(I32), d_word_picked[:].bitcast(I32), 4)
+        warm = ps.tile([P, PICKED], F32, name="acc", bufs=4)
+        for unused in range(2):
+            nc.tensor.matmul_mx(
+                out=warm[:],
+                lhsT=d_word_picked[:, :P].bitcast(FP8X4),
+                lhsT_scale=staged_scales[:, :P],
+                rhs=d_word_picked[:].bitcast(FP8X4),
+                rhs_scale=staged_scales[:, :PICKED],
+                start=True,
+                stop=True,
+            )
 
         def score(bank, t, query_words, j0, width):
             nc.tensor.matmul_mx(
@@ -108,9 +119,10 @@ def tile_picked_sigattn_tanh_po_kernel(
         for width in CHUNKS:
             chunks.append((sum(w for j, w in chunks), width))
 
-        def first(j0, width, per_bank):
+        def first(j0, width, banks):
             th = tile("tanh%d" % j0, [P, PACK, width], F32)
-            for t0 in range(0, PACK, per_bank):
+            for b, per_bank in enumerate(banks):
+                t0 = sum(banks[:b])
                 scores = ps.tile([P, per_bank, width], F32, name="scores", bufs=4)
                 for t in range(per_bank):
                     score(scores[:, t, :], t0 + t, query_halves[j0 // HALF], j0, width)
@@ -171,20 +183,22 @@ def tile_picked_sigattn_tanh_po_kernel(
                 in_=y.rearrange("p t (c i) -> p c t i", i=4),
             )
             nc.vector.quantize_mx(out=out_words[:, j0 : j0 + width].bitcast(FP8X4), scales=out_scales[:, j0 : j0 + width], in_=yb[:])
+            if j0 + width == 384:
+                nc.scalar.dma_start(out_words_hbm[:, :384], out_words[:, :384].bitcast(I32))
             if j0 + width == PICKED:
-                nc.sync.dma_start(out_words_hbm, out_words[:].bitcast(I32))
+                nc.sync.dma_start(out_words_hbm[:, 384:], out_words[:, 384:].bitcast(I32))
 
         n = len(chunks)
         ths = []
         ys = []
-        th = first(0, 128, 2)
+        th = first(0, 128, (1, 1, 2))
         ths.append(th[:])
-        th = first(128, 128, 4)
+        th = first(128, 128, (4,))
         ths.append(th[:])
-        th = first(256, 128, 4)
+        th = first(256, 128, (4,))
         ths.append(th[:])
         ys.append(second(0, weigh(0, ths[0])))
-        th = first(384, 128, 4)
+        th = first(384, 128, (4,))
         for j0, width in chunks[3:]:
             ths.append(th[:, :, j0 - 384 : j0 - 384 + width])
         for c in range(1, n):

@@ -17,7 +17,18 @@ PACK = 4
 TABLE = 2048
 PICKED = 512
 HALF = 256
+LIST_GROUP = 16
+BLOCK_PARTITIONS = 8
+QUADRANT = 32
+LINE_BYTES = 16
+GROUP = 128
 CHUNKS = (128, 128, 128, 64, 64)
+FIRST_BANKS = (1, 1, 2)
+LATER_BANKS = (2, 2)
+SCORE_BANKS = 5
+RESULT_BANKS = 3
+LEAD = 3
+EARLY_WORDS = PICKED - GROUP
 FLOPS = 2 * 2 * 512 * 512 * 512
 
 
@@ -28,10 +39,16 @@ def deal(nc, dst, src, run):
     )
 
 
+def list_half(offsets, h):
+    return offsets[:, h * HALF // LIST_GROUP : (h + 1) * HALF // LIST_GROUP]
+
+
 def tile_picked_sigattn_tanh_po_kernel(
     tc, x_words, x_scales, d_words, d_scales, kb, gn, w1_words, w1_scales, offs, kidx, out_0, out_1, out_2
 ):
     nc = tc.nc
+    byte_run = LINE_BYTES
+    word_run = LINE_BYTES // 4
     with ExitStack() as ctx:
         sb = ctx.enter_context(tc.tile_pool(name="sb", bufs=1))
         ps = ctx.enter_context(tc.psum_pool(name="ps", bufs=1))
@@ -39,8 +56,8 @@ def tile_picked_sigattn_tanh_po_kernel(
         def tile(name, shape, dtype, tag=None):
             return sb.tile(shape, dtype, name=name, tag=tag or name, align_bytes=64)
 
-        kidx_sb = sb.tile([P, PICKED // 16], U16, name="kidx_sb")
-        offs_sb = sb.tile([P, PICKED // 16], U16, name="offs_sb")
+        kidx_sb = sb.tile([P, PICKED // LIST_GROUP], U16, name="kidx_sb")
+        offs_sb = sb.tile([P, PICKED // LIST_GROUP], U16, name="offs_sb")
         d_scale_table = tile("d_scale_table", [P, TABLE], U8)
         x_scale_table = tile("x_scale_table", [P, TABLE], U8)
         d_word_table = tile("d_word_table", [P, TABLE], U32)
@@ -58,9 +75,10 @@ def tile_picked_sigattn_tanh_po_kernel(
         nc.sync.dma_start(offs_sb[:], offs)
         nc.scalar.dma_start(kb_sb[:], kb.rearrange("(p t) o -> p (t o)", t=PACK))
         nc.scalar.dma_start(gn_sb[:], gn.rearrange("(p t) o -> p (t o)", t=PACK))
-        nc.scalar.dma_start(staged_scales[:, 2 * PICKED :].bitcast(I32)[0:P:8, :], w1_scales[0].bitcast(I32))
-        nc.scalar.dma_start(d_scale_table[:].bitcast(I32)[0:P:8, :], d_scales[0].bitcast(I32))
-        nc.scalar.dma_start(x_scale_table[:].bitcast(I32)[0:P:8, :], x_scales[0].bitcast(I32))
+        row_places = slice(0, P, BLOCK_PARTITIONS)
+        nc.scalar.dma_start(staged_scales[:, 2 * PICKED :].bitcast(I32)[row_places, :], w1_scales[0].bitcast(I32))
+        nc.scalar.dma_start(d_scale_table[:].bitcast(I32)[row_places, :], d_scales[0].bitcast(I32))
+        nc.scalar.dma_start(x_scale_table[:].bitcast(I32)[row_places, :], x_scales[0].bitcast(I32))
         nc.scalar.dma_start(d_word_table[:].bitcast(I32), d_words[0].rearrange("p n t -> p (n t)").bitcast(I32))
         nc.scalar.dma_start(x_word_table[:].bitcast(I32), x_words[0].rearrange("p n t -> p (n t)").bitcast(I32))
 
@@ -68,10 +86,13 @@ def tile_picked_sigattn_tanh_po_kernel(
         x_scale_picked = tile("x_scale_picked", [P, PICKED], U8, tag="x_picked")
         nc.vector.tensor_copy(d_scale_picked[:], d_scale_table[:].indirect(kidx_sb[:]))
         nc.vector.tensor_copy(x_scale_picked[:], x_scale_table[:].indirect(offs_sb[:]))
-        deal(nc, staged_scales[:, :PICKED], d_scale_picked[:], 16)
+        deal(nc, staged_scales[:, :PICKED], d_scale_picked[:], byte_run)
         nc.vector.tensor_copy(staged_scales[:, PICKED : 2 * PICKED].bitcast(I32), x_scale_picked[:].bitcast(I32))
-        for r in range(4):
-            nc.sync.dma_start(mx_scales[:].bitcast(I32)[r:P:32, :], staged_scales[:].bitcast(I32)[8 * r : P : 32, :])
+        for r in range(QUADRANT // BLOCK_PARTITIONS):
+            nc.sync.dma_start(
+                mx_scales[:].bitcast(I32)[r:P:QUADRANT, :],
+                staged_scales[:].bitcast(I32)[BLOCK_PARTITIONS * r : P : QUADRANT, :],
+            )
         w_word_in = tile("w_word_in", [P, PICKED], U32, tag="x_picked")
         nc.sync.dma_start(w_word_in[:].bitcast(I32), w1_words[0].rearrange("p n t -> p (n t)").bitcast(I32))
         key_scales = mx_scales[:, :PICKED]
@@ -79,84 +100,78 @@ def tile_picked_sigattn_tanh_po_kernel(
 
         d_word_picked = tile("d_word_picked", [P, PICKED], U32, tag="d_picked")
         key_words = tile("key_words", [P, PICKED], U32)
-        nc.vector.tensor_copy(d_word_picked[:], d_word_table[:].indirect(kidx_sb[:]))
-        deal(nc, key_words[:].bitcast(I32), d_word_picked[:].bitcast(I32), 4)
-        warm = ps.tile([P, PICKED], F32, name="acc", bufs=4)
-        for unused in range(2):
+        for h in range(PICKED // HALF):
+            nc.vector.tensor_copy(d_word_picked[:, h * HALF : (h + 1) * HALF], d_word_table[:].indirect(list_half(kidx_sb, h)))
+        deal(nc, key_words[:].bitcast(I32), d_word_picked[:].bitcast(I32), word_run)
+
+        warm = ps.tile([P, PICKED], F32, name="acc", bufs=RESULT_BANKS)
+        for width in (HALF, HALF, PICKED):
             nc.tensor.matmul_mx(
-                out=warm[:],
+                out=warm[:, :width],
                 lhsT=d_word_picked[:, :P].bitcast(FP8X4),
                 lhsT_scale=staged_scales[:, :P],
-                rhs=d_word_picked[:].bitcast(FP8X4),
-                rhs_scale=staged_scales[:, :PICKED],
+                rhs=d_word_picked[:, :width].bitcast(FP8X4),
+                rhs_scale=staged_scales[:, :width],
                 start=True,
                 stop=True,
             )
 
-        def score(bank, t, query_words, j0, width):
-            nc.tensor.matmul_mx(
-                out=bank,
-                lhsT=key_words[:, t * P : (t + 1) * P].bitcast(FP8X4),
-                lhsT_scale=key_scales[:, t * P : (t + 1) * P],
-                rhs=query_words[:, j0 % HALF : j0 % HALF + width].bitcast(FP8X4),
-                rhs_scale=query_scales[:, j0 : j0 + width],
-                start=True,
-                stop=True,
-            )
-
-        offs_halves = [offs_sb[:, h * HALF // 16 : (h + 1) * HALF // 16] for h in range(2)]
         query_halves = []
         for h in range(PICKED // HALF):
             query_words = tile("query_words%d" % h, [P, HALF], U32)
-            nc.vector.tensor_copy(query_words[:], x_word_table[:].indirect(offs_halves[h]))
+            nc.vector.tensor_copy(query_words[:], x_word_table[:].indirect(list_half(offs_sb, h)))
             query_halves.append(query_words)
         value_words = tile("value_words", [P, PICKED], U32, tag="d_picked")
         value_scales = tile("value_scales", [P, PICKED], U8)
-        deal(nc, value_scales[:], mx_scales[:, 2 * PICKED :], 16)
-        deal(nc, value_words[:].bitcast(I32), w_word_in[:].bitcast(I32), 4)
+        deal(nc, value_scales[:], mx_scales[:, 2 * PICKED :], byte_run)
+        deal(nc, value_words[:].bitcast(I32), w_word_in[:].bitcast(I32), word_run)
 
-        chunks = []
-        for width in CHUNKS:
-            chunks.append((sum(w for j, w in chunks), width))
-
-        def first(j0, width, banks):
-            th = tile("tanh%d" % j0, [P, PACK, width], F32)
-            for b, per_bank in enumerate(banks):
-                t0 = sum(banks[:b])
-                scores = ps.tile([P, per_bank, width], F32, name="scores", bufs=4)
-                for t in range(per_bank):
-                    score(scores[:, t, :], t0 + t, query_halves[j0 // HALF], j0, width)
-                for t in range(per_bank):
-                    nc.scalar.activation(
-                        out=th[:, t0 + t, :], in_=scores[:, t, :], func=ACT.Tanh, bias=kb_sb[:, t0 + t : t0 + t + 1], scale=0.0625
-                    )
-            return th
-
+        chunk_starts = [sum(CHUNKS[:c]) for c in range(len(CHUNKS))]
         out_rows = out_0.rearrange("(p t) j -> p t j", t=PACK)
         out_words_hbm = out_1[0].rearrange("p n t -> p (n t)").bitcast(I32)
         out_scales = tile("out_scales", [P, PICKED], U8)
-
         out_words = tile("out_words", [P, PICKED], U32)
 
-        def weigh(c, th):
-            j0, width = chunks[c]
-            z = tile("z%d" % c, [P, width * PACK], BF16)
-            nc.vector.tensor_tensor(
-                out=z[:].rearrange("p (c i t) -> p c t i", t=PACK, i=4),
-                in0=th.rearrange("p t (c i) -> p c t i", i=4),
-                in1=gn_sb[:].unsqueeze(1).unsqueeze(3).to_broadcast([P, width // 4, PACK, 4]),
-                op=ALU.mult,
-            )
-            return z
+        def tanh_group(g):
+            j0 = g * GROUP
+            banks = FIRST_BANKS if g == 0 else LATER_BANKS
+            th = tile("tanh%d" % j0, [P, PACK, GROUP], F32)
+            for b, per_bank in enumerate(banks):
+                t0 = sum(banks[:b])
+                scores = ps.tile([P, per_bank, GROUP], F32, name="scores", bufs=SCORE_BANKS)
+                for t in range(t0, t0 + per_bank):
+                    nc.tensor.matmul_mx(
+                        out=scores[:, t - t0, :],
+                        lhsT=key_words[:, t * P : (t + 1) * P].bitcast(FP8X4),
+                        lhsT_scale=key_scales[:, t * P : (t + 1) * P],
+                        rhs=query_halves[j0 // HALF][:, j0 % HALF : j0 % HALF + GROUP].bitcast(FP8X4),
+                        rhs_scale=query_scales[:, j0 : j0 + GROUP],
+                        start=True,
+                        stop=True,
+                    )
+                for t in range(t0, t0 + per_bank):
+                    nc.scalar.activation(
+                        out=th[:, t, :], in_=scores[:, t - t0, :], func=ACT.Tanh, bias=kb_sb[:, t : t + 1], scale=0.0625
+                    )
+            return th
 
+        tanh_tiles = []
         y_tiles = []
 
-        def second(c, z):
-            j0, width = chunks[c]
+        def second_product(c):
+            j0, width = chunk_starts[c], CHUNKS[c]
+            in_group = slice(j0 % GROUP, j0 % GROUP + width)
+            z = tile("z%d" % c, [P, width * PACK], BF16)
+            nc.vector.tensor_tensor(
+                out=z[:].rearrange("p (c i t) -> p c t i", t=PACK, i=word_run),
+                in0=tanh_tiles[j0 // GROUP][:, :, in_group].rearrange("p t (c i) -> p c t i", i=word_run),
+                in1=gn_sb[:].unsqueeze(1).unsqueeze(3).to_broadcast([P, width // word_run, PACK, word_run]),
+                op=ALU.mult,
+            )
             z_words = tile("z_words%d" % c, [P, width], U32)
             z_scales = tile("z_scales%d" % c, [P, width], U8)
             nc.vector.quantize_mx(out=z_words[:].bitcast(FP8X4), scales=z_scales[:], in_=z[:])
-            acc = ps.tile([P, PACK, width], F32, name="acc", bufs=4)
+            acc = ps.tile([P, PACK, width], F32, name="acc", bufs=RESULT_BANKS)
             for t in range(PACK):
                 nc.tensor.matmul_mx(
                     out=acc[:, t, :],
@@ -167,44 +182,40 @@ def tile_picked_sigattn_tanh_po_kernel(
                     start=True,
                     stop=True,
                 )
-            if j0 % P == 0:
-                y_tiles.append(tile("y%d" % c, [P, PACK, P], F32))
-            y = y_tiles[-1][:, :, j0 % P : j0 % P + width]
-            yb = tile("yb%d" % c, [P, width * PACK], BF16)
-            nc.scalar.copy(out=y, in_=acc[:])
-            if (j0 + width) % P == 0:
-                nc.sync.dma_start(out_rows[:, :, j0 + width - P : j0 + width], y_tiles[-1][:])
-            return y, yb
+            if j0 % GROUP == 0:
+                y_tiles.append(tile("y%d" % c, [P, PACK, GROUP], F32))
+            y_rounded = tile("yb%d" % c, [P, width * PACK], BF16)
+            nc.scalar.copy(out=y_tiles[-1][:, :, in_group], in_=acc[:])
+            if (j0 + width) % GROUP == 0:
+                nc.sync.dma_start(out_rows[:, :, j0 + width - GROUP : j0 + width], y_tiles[-1][:])
+            return y_tiles[-1][:, :, in_group], y_rounded
 
-        def planes(c, y, yb):
-            j0, width = chunks[c]
+        def planes(c, y, y_rounded):
+            j0, j1 = chunk_starts[c], chunk_starts[c] + CHUNKS[c]
             nc.vector.tensor_copy(
-                out=yb[:].rearrange("p (c i t) -> p c t i", t=PACK, i=4),
-                in_=y.rearrange("p t (c i) -> p c t i", i=4),
+                out=y_rounded[:].rearrange("p (c i t) -> p c t i", t=PACK, i=word_run),
+                in_=y.rearrange("p t (c i) -> p c t i", i=word_run),
             )
-            nc.vector.quantize_mx(out=out_words[:, j0 : j0 + width].bitcast(FP8X4), scales=out_scales[:, j0 : j0 + width], in_=yb[:])
-            if j0 + width == 384:
-                nc.scalar.dma_start(out_words_hbm[:, :384], out_words[:, :384].bitcast(I32))
-            if j0 + width == PICKED:
-                nc.sync.dma_start(out_words_hbm[:, 384:], out_words[:, 384:].bitcast(I32))
+            nc.vector.quantize_mx(out=out_words[:, j0:j1].bitcast(FP8X4), scales=out_scales[:, j0:j1], in_=y_rounded[:])
+            if j1 == EARLY_WORDS:
+                nc.scalar.dma_start(out_words_hbm[:, :EARLY_WORDS], out_words[:, :EARLY_WORDS].bitcast(I32))
+            if j1 == PICKED:
+                nc.sync.dma_start(out_words_hbm[:, EARLY_WORDS:], out_words[:, EARLY_WORDS:].bitcast(I32))
 
-        n = len(chunks)
-        ths = []
-        ys = []
-        th = first(0, 128, (1, 1, 2))
-        ths.append(th[:])
-        th = first(128, 128, (4,))
-        ths.append(th[:])
-        th = first(256, 128, (4,))
-        ths.append(th[:])
-        ys.append(second(0, weigh(0, ths[0])))
-        th = first(384, 128, (4,))
-        for j0, width in chunks[3:]:
-            ths.append(th[:, :, j0 - 384 : j0 - 384 + width])
-        for c in range(1, n):
-            ys.append(second(c, weigh(c, ths[c])))
-        for c in range(n):
-            planes(c, *ys[c])
-        for q in range(4):
-            eng = nc.scalar if q % 2 == 0 else nc.sync
-            eng.dma_start(out_2[0].bitcast(I32)[4 * q : 4 * q + 4, :], out_scales[:].bitcast(I32)[32 * q : 32 * q + 4, :])
+        for g in range(LEAD):
+            tanh_tiles.append(tanh_group(g))
+        results = [second_product(0)]
+        for g in range(LEAD, PICKED // GROUP):
+            tanh_tiles.append(tanh_group(g))
+        for c in range(1, len(CHUNKS)):
+            results.append(second_product(c))
+        for c in range(len(CHUNKS)):
+            planes(c, *results[c])
+
+        rows = QUADRANT // BLOCK_PARTITIONS
+        for q in range(P // QUADRANT):
+            queue = nc.scalar if q % 2 == 0 else nc.sync
+            queue.dma_start(
+                out_2[0].bitcast(I32)[rows * q : rows * (q + 1), :],
+                out_scales[:].bitcast(I32)[QUADRANT * q : QUADRANT * q + rows, :],
+            )

@@ -104,18 +104,6 @@ def tile_picked_sigattn_tanh_po_kernel(
             nc.vector.tensor_copy(d_word_picked[:, h * HALF : (h + 1) * HALF], d_word_table[:].indirect(list_half(kidx_sb, h)))
         deal(nc, key_words[:].bitcast(I32), d_word_picked[:].bitcast(I32), word_run)
 
-        warm = ps.tile([P, PICKED], F32, name="acc", bufs=RESULT_BANKS)
-        for width in (HALF, HALF, PICKED):
-            nc.tensor.matmul_mx(
-                out=warm[:, :width],
-                lhsT=d_word_picked[:, :P].bitcast(FP8X4),
-                lhsT_scale=staged_scales[:, :P],
-                rhs=d_word_picked[:, :width].bitcast(FP8X4),
-                rhs_scale=staged_scales[:, :width],
-                start=True,
-                stop=True,
-            )
-
         query_halves = []
         for h in range(PICKED // HALF):
             query_words = tile("query_words%d" % h, [P, HALF], U32)

@@ -16,7 +16,6 @@ P = 128
 PACK = 4
 TABLE = 2048
 PICKED = 512
-HALF = 256
 LIST_GROUP = 16
 BLOCK_PARTITIONS = 8
 QUADRANT = 32
@@ -29,6 +28,7 @@ SCORE_BANKS = 5
 RESULT_BANKS = 3
 LEAD = 3
 EARLY_WORDS = PICKED - GROUP
+QUERY_GATHERS = (GROUP, PICKED - GROUP)
 FLOPS = 2 * 2 * 512 * 512 * 512
 
 
@@ -39,8 +39,8 @@ def deal(nc, dst, src, run):
     )
 
 
-def list_half(offsets, h):
-    return offsets[:, h * HALF // LIST_GROUP : (h + 1) * HALF // LIST_GROUP]
+def list_part(offsets, start, count):
+    return offsets[:, start // LIST_GROUP : (start + count) // LIST_GROUP]
 
 
 def tile_picked_sigattn_tanh_po_kernel(
@@ -100,15 +100,16 @@ def tile_picked_sigattn_tanh_po_kernel(
 
         d_word_picked = tile("d_word_picked", [P, PICKED], U32, tag="d_picked")
         key_words = tile("key_words", [P, PICKED], U32)
-        for h in range(PICKED // HALF):
-            nc.vector.tensor_copy(d_word_picked[:, h * HALF : (h + 1) * HALF], d_word_table[:].indirect(list_half(kidx_sb, h)))
+        nc.vector.tensor_copy(d_word_picked[:], d_word_table[:].indirect(kidx_sb[:]))
         deal(nc, key_words[:].bitcast(I32), d_word_picked[:].bitcast(I32), word_run)
 
-        query_halves = []
-        for h in range(PICKED // HALF):
-            query_words = tile("query_words%d" % h, [P, HALF], U32)
-            nc.vector.tensor_copy(query_words[:], x_word_table[:].indirect(list_half(offs_sb, h)))
-            query_halves.append(query_words)
+        query_groups = []
+        first = 0
+        for width in QUERY_GATHERS:
+            query_words = tile("query_words%d" % first, [P, width], U32)
+            nc.vector.tensor_copy(query_words[:], x_word_table[:].indirect(list_part(offs_sb, first, width)))
+            query_groups.extend(query_words[:, j : j + GROUP] for j in range(0, width, GROUP))
+            first = first + width
         value_words = tile("value_words", [P, PICKED], U32, tag="d_picked")
         value_scales = tile("value_scales", [P, PICKED], U8)
         deal(nc, value_scales[:], mx_scales[:, 2 * PICKED :], byte_run)
@@ -132,7 +133,7 @@ def tile_picked_sigattn_tanh_po_kernel(
                         out=scores[:, t - t0, :],
                         lhsT=key_words[:, t * P : (t + 1) * P].bitcast(FP8X4),
                         lhsT_scale=key_scales[:, t * P : (t + 1) * P],
-                        rhs=query_halves[j0 // HALF][:, j0 % HALF : j0 % HALF + GROUP].bitcast(FP8X4),
+                        rhs=query_groups[g].bitcast(FP8X4),
                         rhs_scale=query_scales[:, j0 : j0 + GROUP],
                         start=True,
                         stop=True,

@@ -58,8 +58,8 @@ def tile_picked_sigattn_tanh_po_kernel(
 
         kidx_sb = sb.tile([P, PICKED // LIST_GROUP], U16, name="kidx_sb")
         offs_sb = sb.tile([P, PICKED // LIST_GROUP], U16, name="offs_sb")
-        d_scale_table = tile("d_scale_table", [P, TABLE], U8)
-        x_scale_table = tile("x_scale_table", [P, TABLE], U8)
+        d_scale_table = tile("d_scale_table", [P, TABLE], U8, tag="x_picked")
+        x_scale_table = tile("x_scale_table", [P, TABLE], U8, tag="d_words")
         d_word_table = tile("d_word_table", [P, TABLE], U32)
         x_word_table = tile("x_word_table", [P, TABLE], U32)
         mx_scales = tile("mx_scales", [P, 3 * PICKED], U8)
@@ -78,11 +78,11 @@ def tile_picked_sigattn_tanh_po_kernel(
         row_places = slice(0, P, BLOCK_PARTITIONS)
         nc.scalar.dma_start(staged_scales[:, 2 * PICKED :].bitcast(I32)[row_places, :], w1_scales[0].bitcast(I32))
         nc.scalar.dma_start(d_scale_table[:].bitcast(I32)[row_places, :], d_scales[0].bitcast(I32))
-        nc.scalar.dma_start(x_scale_table[:].bitcast(I32)[row_places, :], x_scales[0].bitcast(I32))
+        nc.sync.dma_start(x_scale_table[:].bitcast(I32)[row_places, :], x_scales[0].bitcast(I32))
         nc.scalar.dma_start(d_word_table[:].bitcast(I32), d_words[0].rearrange("p n t -> p (n t)").bitcast(I32))
         nc.scalar.dma_start(x_word_table[:].bitcast(I32), x_words[0].rearrange("p n t -> p (n t)").bitcast(I32))
 
-        d_scale_picked = tile("d_scale_picked", [P, PICKED], U8, tag="d_picked")
+        d_scale_picked = tile("d_scale_picked", [P, PICKED], U8)
         x_scale_picked = tile("x_scale_picked", [P, PICKED], U8, tag="x_picked")
         nc.vector.tensor_copy(d_scale_picked[:], d_scale_table[:].indirect(kidx_sb[:]))
         nc.vector.tensor_copy(x_scale_picked[:], x_scale_table[:].indirect(offs_sb[:]))
@@ -98,7 +98,7 @@ def tile_picked_sigattn_tanh_po_kernel(
         key_scales = mx_scales[:, :PICKED]
         query_scales = mx_scales[:, PICKED : 2 * PICKED]
 
-        d_word_picked = tile("d_word_picked", [P, PICKED], U32, tag="d_picked")
+        d_word_picked = tile("d_word_picked", [P, PICKED], U32, tag="d_words")
         key_words = tile("key_words", [P, PICKED], U32)
         nc.vector.tensor_copy(d_word_picked[:], d_word_table[:].indirect(kidx_sb[:]))
         deal(nc, key_words[:].bitcast(I32), d_word_picked[:].bitcast(I32), word_run)
@@ -110,7 +110,7 @@ def tile_picked_sigattn_tanh_po_kernel(
             nc.vector.tensor_copy(query_words[:], x_word_table[:].indirect(list_part(offs_sb, first, width)))
             query_groups.extend(query_words[:, j : j + GROUP] for j in range(0, width, GROUP))
             first = first + width
-        value_words = tile("value_words", [P, PICKED], U32, tag="d_picked")
+        value_words = tile("value_words", [P, PICKED], U32, tag="d_words")
         value_scales = tile("value_scales", [P, PICKED], U8)
         deal(nc, value_scales[:], mx_scales[:, 2 * PICKED :], byte_run)
         deal(nc, value_words[:].bitcast(I32), w_word_in[:].bitcast(I32), word_run)

@@ -58,7 +58,7 @@ def tile_picked_sigattn_tanh_po_kernel(
 
         kidx_sb = sb.tile([P, PICKED // LIST_GROUP], U16, name="kidx_sb")
         offs_sb = sb.tile([P, PICKED // LIST_GROUP], U16, name="offs_sb")
-        d_scale_table = tile("d_scale_table", [P, TABLE], U8, tag="x_picked")
+        d_scale_table = tile("d_scale_table", [P, TABLE], U8)
         x_scale_table = tile("x_scale_table", [P, TABLE], U8, tag="d_words")
         d_word_table = tile("d_word_table", [P, TABLE], U32)
         x_word_table = tile("x_word_table", [P, TABLE], U32)
@@ -76,9 +76,9 @@ def tile_picked_sigattn_tanh_po_kernel(
         nc.scalar.dma_start(kb_sb[:], kb.rearrange("(p t) o -> p (t o)", t=PACK))
         nc.scalar.dma_start(gn_sb[:], gn.rearrange("(p t) o -> p (t o)", t=PACK))
         row_places = slice(0, P, BLOCK_PARTITIONS)
-        nc.scalar.dma_start(staged_scales[:, 2 * PICKED :].bitcast(I32)[row_places, :], w1_scales[0].bitcast(I32))
         nc.scalar.dma_start(d_scale_table[:].bitcast(I32)[row_places, :], d_scales[0].bitcast(I32))
         nc.sync.dma_start(x_scale_table[:].bitcast(I32)[row_places, :], x_scales[0].bitcast(I32))
+        nc.sync.dma_start(staged_scales[:, 2 * PICKED :].bitcast(I32)[row_places, :], w1_scales[0].bitcast(I32))
         nc.scalar.dma_start(d_word_table[:].bitcast(I32), d_words[0].rearrange("p n t -> p (n t)").bitcast(I32))
         nc.scalar.dma_start(x_word_table[:].bitcast(I32), x_words[0].rearrange("p n t -> p (n t)").bitcast(I32))
 

@@ -51,6 +51,7 @@ def tile_picked_sigattn_tanh_po_kernel(
     word_run = LINE_BYTES // 4
     with ExitStack() as ctx:
         sb = ctx.enter_context(tc.tile_pool(name="sb", bufs=1))
+        shared = ctx.enter_context(tc.tile_pool(name="shared", bufs=1))
         ps = ctx.enter_context(tc.psum_pool(name="ps", bufs=1))
 
         def tile(name, shape, dtype, tag=None):
@@ -61,7 +62,7 @@ def tile_picked_sigattn_tanh_po_kernel(
         d_scale_table = tile("d_scale_table", [P, TABLE], U8)
         x_scale_table = tile("x_scale_table", [P, TABLE], U8, tag="d_words")
         d_word_table = tile("d_word_table", [P, TABLE], U32)
-        x_word_table = tile("x_word_table", [P, TABLE], U32)
+        x_word_table = shared.tile([P, TABLE], U32, name="x_word_table", align_bytes=64, offset=0)
         mx_scales = tile("mx_scales", [P, 3 * PICKED], U8)
         kb_sb = tile("kb_sb", [P, PACK], F32)
         gn_sb = tile("gn_sb", [P, PACK], F32)
@@ -77,8 +78,8 @@ def tile_picked_sigattn_tanh_po_kernel(
         nc.scalar.dma_start(gn_sb[:], gn.rearrange("(p t) o -> p (t o)", t=PACK))
         row_places = slice(0, P, BLOCK_PARTITIONS)
         nc.scalar.dma_start(d_scale_table[:].bitcast(I32)[row_places, :], d_scales[0].bitcast(I32))
-        nc.sync.dma_start(x_scale_table[:].bitcast(I32)[row_places, :], x_scales[0].bitcast(I32))
-        nc.sync.dma_start(staged_scales[:, 2 * PICKED :].bitcast(I32)[row_places, :], w1_scales[0].bitcast(I32))
+        nc.scalar.dma_start(x_scale_table[:].bitcast(I32)[row_places, :], x_scales[0].bitcast(I32))
+        nc.scalar.dma_start(staged_scales[:, 2 * PICKED :].bitcast(I32)[row_places, :], w1_scales[0].bitcast(I32))
         nc.scalar.dma_start(d_word_table[:].bitcast(I32), d_words[0].rearrange("p n t -> p (n t)").bitcast(I32))
         nc.scalar.dma_start(x_word_table[:].bitcast(I32), x_words[0].rearrange("p n t -> p (n t)").bitcast(I32))
 
@@ -110,8 +111,8 @@ def tile_picked_sigattn_tanh_po_kernel(
             nc.vector.tensor_copy(query_words[:], x_word_table[:].indirect(list_part(offs_sb, first, width)))
             query_groups.extend(query_words[:, j : j + GROUP] for j in range(0, width, GROUP))
             first = first + width
-        value_words = tile("value_words", [P, PICKED], U32, tag="d_words")
-        value_scales = tile("value_scales", [P, PICKED], U8)
+        value_words = shared.tile([P, PICKED], U32, name="value_words", align_bytes=64, offset=0)
+        value_scales = shared.tile([P, PICKED], U8, name="value_scales", align_bytes=64, offset=4 * PICKED)
         deal(nc, value_scales[:], mx_scales[:, 2 * PICKED :], byte_run)
         deal(nc, value_words[:].bitcast(I32), w_word_in[:].bitcast(I32), word_run)
 

@@ -63,36 +63,37 @@ def tile_picked_sigattn_tanh_po_kernel(
         x_scale_table = tile("x_scale_table", [P, TABLE], U8, tag="d_words")
         d_word_table = tile("d_word_table", [P, TABLE], U32)
         x_word_table = shared.tile([P, TABLE], U32, name="x_word_table", align_bytes=64, offset=0)
-        mx_scales = tile("mx_scales", [P, 3 * PICKED], U8)
         kb_sb = tile("kb_sb", [P, PACK], F32)
         gn_sb = tile("gn_sb", [P, PACK], F32)
 
-        staged_scales = tile("staged_scales", [P, 3 * PICKED], U8)
+        mx_scales = tile("mx_scales", [P, 3 * PICKED], U8)
         nc.vector.memset(d_scale_table[:].bitcast(I32), 0)
-        nc.gpsimd.memset(x_scale_table[:].bitcast(I32), 0)
-        nc.vector.memset(mx_scales[:].bitcast(I32), 0)
+        nc.vector.memset(x_scale_table[:].bitcast(I32), 0)
+        nc.vector.memset(mx_scales[:, 2 * PICKED :].bitcast(I32), 0)
 
         nc.sync.dma_start(kidx_sb[:], kidx)
         nc.sync.dma_start(offs_sb[:], offs)
-        nc.scalar.dma_start(kb_sb[:], kb.rearrange("(p t) o -> p (t o)", t=PACK))
-        nc.scalar.dma_start(gn_sb[:], gn.rearrange("(p t) o -> p (t o)", t=PACK))
+        d_words_hbm = d_words[0].rearrange("p n t -> p (n t)").bitcast(I32)
         row_places = slice(0, P, BLOCK_PARTITIONS)
+        nc.scalar.dma_start(d_word_table[:, :256].bitcast(I32), d_words_hbm[:, :256])
         nc.scalar.dma_start(d_scale_table[:].bitcast(I32)[row_places, :], d_scales[0].bitcast(I32))
+        nc.scalar.dma_start(kb_sb[:], kb.rearrange("(p t) o -> p (t o)", t=PACK))
         nc.scalar.dma_start(x_scale_table[:].bitcast(I32)[row_places, :], x_scales[0].bitcast(I32))
-        nc.scalar.dma_start(staged_scales[:, 2 * PICKED :].bitcast(I32)[row_places, :], w1_scales[0].bitcast(I32))
-        nc.scalar.dma_start(d_word_table[:].bitcast(I32), d_words[0].rearrange("p n t -> p (n t)").bitcast(I32))
+        nc.scalar.dma_start(mx_scales[:, 2 * PICKED :].bitcast(I32)[row_places, :], w1_scales[0].bitcast(I32))
+        nc.scalar.dma_start(d_word_table[:, 256:].bitcast(I32), d_words_hbm[:, 256:])
         nc.scalar.dma_start(x_word_table[:].bitcast(I32), x_words[0].rearrange("p n t -> p (n t)").bitcast(I32))
+        nc.scalar.dma_start(gn_sb[:], gn.rearrange("(p t) o -> p (t o)", t=PACK))
 
         d_scale_picked = tile("d_scale_picked", [P, PICKED], U8)
         x_scale_picked = tile("x_scale_picked", [P, PICKED], U8, tag="x_picked")
         nc.vector.tensor_copy(d_scale_picked[:], d_scale_table[:].indirect(kidx_sb[:]))
         nc.vector.tensor_copy(x_scale_picked[:], x_scale_table[:].indirect(offs_sb[:]))
-        deal(nc, staged_scales[:, :PICKED], d_scale_picked[:], byte_run)
-        nc.vector.tensor_copy(staged_scales[:, PICKED : 2 * PICKED].bitcast(I32), x_scale_picked[:].bitcast(I32))
-        for r in range(QUADRANT // BLOCK_PARTITIONS):
+        deal(nc, mx_scales[:, :PICKED], d_scale_picked[:], byte_run)
+        nc.vector.tensor_copy(mx_scales[:, PICKED : 2 * PICKED].bitcast(I32), x_scale_picked[:].bitcast(I32))
+        for r in range(1, QUADRANT // BLOCK_PARTITIONS):
             nc.sync.dma_start(
                 mx_scales[:].bitcast(I32)[r:P:QUADRANT, :],
-                staged_scales[:].bitcast(I32)[BLOCK_PARTITIONS * r : P : QUADRANT, :],
+                mx_scales[:].bitcast(I32)[BLOCK_PARTITIONS * r : P : QUADRANT, :],
             )
         w_word_in = tile("w_word_in", [P, PICKED], U32, tag="x_picked")
         nc.sync.dma_start(w_word_in[:].bitcast(I32), w1_words[0].rearrange("p n t -> p (n t)").bitcast(I32))

@@ -20,15 +20,13 @@ LIST_GROUP = 16
 BLOCK_PARTITIONS = 8
 QUADRANT = 32
 LINE_BYTES = 16
-GROUP = 128
-CHUNKS = (128, 128, 128, 64, 64)
+STORE = 128
+GROUPS = (128, 128, 128, 128)
 FIRST_BANKS = (1, 1, 2)
 LATER_BANKS = (2, 2)
 SCORE_BANKS = 5
 RESULT_BANKS = 3
-LEAD = 3
-EARLY_WORDS = PICKED - GROUP
-QUERY_GATHERS = (GROUP, PICKED - GROUP)
+QUERY_GATHERS = (GROUPS[0], PICKED - GROUPS[0])
 FLOPS = 2 * 2 * 512 * 512 * 512
 
 
@@ -105,38 +103,38 @@ def tile_picked_sigattn_tanh_po_kernel(
         nc.vector.tensor_copy(d_word_picked[:], d_word_table[:].indirect(kidx_sb[:]))
         deal(nc, key_words[:].bitcast(I32), d_word_picked[:].bitcast(I32), word_run)
 
-        query_groups = []
-        first = 0
-        for width in QUERY_GATHERS:
-            query_words = tile("query_words%d" % first, [P, width], U32)
-            nc.vector.tensor_copy(query_words[:], x_word_table[:].indirect(list_part(offs_sb, first, width)))
-            query_groups.extend(query_words[:, j : j + GROUP] for j in range(0, width, GROUP))
-            first = first + width
+        early, late = QUERY_GATHERS
+        early_words = tile("early_words", [P, early], U32)
+        late_words = tile("late_words", [P, late], U32)
+        nc.vector.tensor_copy(early_words[:], x_word_table[:].indirect(list_part(offs_sb, 0, early)))
+        nc.vector.tensor_copy(late_words[:], x_word_table[:].indirect(list_part(offs_sb, early, late)))
+        query_groups = [early_words[:]]
+        for g in range(1, len(GROUPS)):
+            query_groups.append(late_words[:, sum(GROUPS[1:g]) : sum(GROUPS[1 : g + 1])])
         value_words = shared.tile([P, PICKED], U32, name="value_words", align_bytes=64, offset=0)
         value_scales = shared.tile([P, PICKED], U8, name="value_scales", align_bytes=64, offset=4 * PICKED)
         deal(nc, value_scales[:], mx_scales[:, 2 * PICKED :], byte_run)
         deal(nc, value_words[:].bitcast(I32), w_word_in[:].bitcast(I32), word_run)
 
-        chunk_starts = [sum(CHUNKS[:c]) for c in range(len(CHUNKS))]
         out_rows = out_0.rearrange("(p t) j -> p t j", t=PACK)
         out_words_hbm = out_1[0].rearrange("p n t -> p (n t)").bitcast(I32)
         out_scales = tile("out_scales", [P, PICKED], U8)
         out_words = tile("out_words", [P, PICKED], U32)
 
         def tanh_group(g):
-            j0 = g * GROUP
+            j0, width = sum(GROUPS[:g]), GROUPS[g]
             banks = FIRST_BANKS if g == 0 else LATER_BANKS
-            th = tile("tanh%d" % j0, [P, PACK, GROUP], F32)
+            th = tile("tanh%d" % j0, [P, PACK, width], F32)
             for b, per_bank in enumerate(banks):
                 t0 = sum(banks[:b])
-                scores = ps.tile([P, per_bank, GROUP], F32, name="scores", bufs=SCORE_BANKS)
+                scores = ps.tile([P, per_bank, width], F32, name="scores", bufs=SCORE_BANKS)
                 for t in range(t0, t0 + per_bank):
                     nc.tensor.matmul_mx(
                         out=scores[:, t - t0, :],
                         lhsT=key_words[:, t * P : (t + 1) * P].bitcast(FP8X4),
                         lhsT_scale=key_scales[:, t * P : (t + 1) * P],
                         rhs=query_groups[g].bitcast(FP8X4),
-                        rhs_scale=query_scales[:, j0 : j0 + GROUP],
+                        rhs_scale=query_scales[:, j0 : j0 + width],
                         start=True,
                         stop=True,
                     )
@@ -146,21 +144,19 @@ def tile_picked_sigattn_tanh_po_kernel(
                     )
             return th
 
-        tanh_tiles = []
-        y_tiles = []
-
-        def second_product(c):
-            j0, width = chunk_starts[c], CHUNKS[c]
-            in_group = slice(j0 % GROUP, j0 % GROUP + width)
-            z = tile("z%d" % c, [P, width * PACK], BF16)
+        def weigh(j0, width, th):
+            z = tile("z%d" % j0, [P, width * PACK], BF16)
             nc.vector.tensor_tensor(
                 out=z[:].rearrange("p (c i t) -> p c t i", t=PACK, i=word_run),
-                in0=tanh_tiles[j0 // GROUP][:, :, in_group].rearrange("p t (c i) -> p c t i", i=word_run),
+                in0=th.rearrange("p t (c i) -> p c t i", i=word_run),
                 in1=gn_sb[:].unsqueeze(1).unsqueeze(3).to_broadcast([P, width // word_run, PACK, word_run]),
                 op=ALU.mult,
             )
-            z_words = tile("z_words%d" % c, [P, width], U32)
-            z_scales = tile("z_scales%d" % c, [P, width], U8)
+            return z
+
+        def second_product(j0, width, z):
+            z_words = tile("z_words%d" % j0, [P, width], U32)
+            z_scales = tile("z_scales%d" % j0, [P, width], U8)
             nc.vector.quantize_mx(out=z_words[:].bitcast(FP8X4), scales=z_scales[:], in_=z[:])
             acc = ps.tile([P, PACK, width], F32, name="acc", bufs=RESULT_BANKS)
             for t in range(PACK):
@@ -173,35 +169,54 @@ def tile_picked_sigattn_tanh_po_kernel(
                     start=True,
                     stop=True,
                 )
-            if j0 % GROUP == 0:
-                y_tiles.append(tile("y%d" % c, [P, PACK, GROUP], F32))
-            y_rounded = tile("yb%d" % c, [P, width * PACK], BF16)
-            nc.scalar.copy(out=y_tiles[-1][:, :, in_group], in_=acc[:])
-            if (j0 + width) % GROUP == 0:
-                nc.sync.dma_start(out_rows[:, :, j0 + width - GROUP : j0 + width], y_tiles[-1][:])
-            return y_tiles[-1][:, :, in_group], y_rounded
+            return acc
 
-        def planes(c, y, y_rounded):
-            j0, j1 = chunk_starts[c], chunk_starts[c] + CHUNKS[c]
+        def round_sbuf(j0, width, y):
+            rounded = tile("yb%d" % j0, [P, width * PACK], BF16)
             nc.vector.tensor_copy(
-                out=y_rounded[:].rearrange("p (c i t) -> p c t i", t=PACK, i=word_run),
+                out=rounded[:].rearrange("p (c i t) -> p c t i", t=PACK, i=word_run),
                 in_=y.rearrange("p t (c i) -> p c t i", i=word_run),
             )
-            nc.vector.quantize_mx(out=out_words[:, j0:j1].bitcast(FP8X4), scales=out_scales[:, j0:j1], in_=y_rounded[:])
-            if j1 == EARLY_WORDS:
-                nc.scalar.dma_start(out_words_hbm[:, :EARLY_WORDS], out_words[:, :EARLY_WORDS].bitcast(I32))
-            if j1 == PICKED:
-                nc.sync.dma_start(out_words_hbm[:, EARLY_WORDS:], out_words[:, EARLY_WORDS:].bitcast(I32))
+            return rounded
 
-        for g in range(LEAD):
-            tanh_tiles.append(tanh_group(g))
-        results = [second_product(0)]
-        for g in range(LEAD, PICKED // GROUP):
-            tanh_tiles.append(tanh_group(g))
-        for c in range(1, len(CHUNKS)):
-            results.append(second_product(c))
-        for c in range(len(CHUNKS)):
-            planes(c, *results[c])
+        def round_psum(j0, width, acc):
+            rounded = tile("yb%d" % j0, [P, width * PACK], BF16)
+            nc.scalar.copy(out=rounded[:].rearrange("p (j t) -> p j t", t=PACK), in_=acc[:].rearrange("p t j -> p j t"))
+            return rounded
+
+        def planes(j0, width, rounded):
+            cols = slice(j0, j0 + width)
+            nc.vector.quantize_mx(out=out_words[:, cols].bitcast(FP8X4), scales=out_scales[:, cols], in_=rounded[:])
+
+        def store_rows(j0, y):
+            nc.sync.dma_start(out_rows[:, :, j0 : j0 + STORE], y[:])
+
+        def store_words(queue, j0, j1):
+            queue.dma_start(out_words_hbm[:, j0:j1], out_words[:, j0:j1].bitcast(I32))
+
+        th = [tanh_group(g) for g in range(3)]
+        y = [tile("y%d" % c, [P, PACK, STORE], F32) for c in range(PICKED // STORE)]
+        half = STORE // 2
+        acc0 = second_product(0, STORE, weigh(0, STORE, th[0][:]))
+        nc.scalar.copy(out=y[0][:], in_=acc0[:])
+        store_rows(0, y[0])
+        th.append(tanh_group(3))
+        for c in (1, 2):
+            acc = second_product(c * STORE, STORE, weigh(c * STORE, STORE, th[c][:]))
+            nc.scalar.copy(out=y[c][:], in_=acc[:])
+            store_rows(c * STORE, y[c])
+        acc3 = second_product(3 * STORE, half, weigh(3 * STORE, half, th[3][:, :, :half]))
+        nc.scalar.copy(out=y[3][:, :, :half], in_=acc3[:])
+        acc4 = second_product(3 * STORE + half, half, weigh(3 * STORE + half, half, th[3][:, :, half:]))
+        rounded4 = round_psum(3 * STORE + half, half, acc4)
+        nc.scalar.copy(out=y[3][:, :, half:], in_=acc4[:])
+        store_rows(3 * STORE, y[3])
+        for c in range(3):
+            planes(c * STORE, STORE, round_sbuf(c * STORE, STORE, y[c][:]))
+        store_words(nc.scalar, 0, 3 * STORE)
+        planes(3 * STORE, half, round_sbuf(3 * STORE, half, y[3][:, :, :half]))
+        planes(3 * STORE + half, half, rounded4)
+        store_words(nc.sync, 3 * STORE, PICKED)
 
         rows = QUADRANT // BLOCK_PARTITIONS
         for q in range(P // QUADRANT):

@@ -206,15 +206,16 @@ def tile_picked_sigattn_tanh_po_kernel(
             nc.scalar.copy(out=y[c][:], in_=acc[:])
             store_rows(c * STORE, y[c])
         acc3 = second_product(3 * STORE, half, weigh(3 * STORE, half, th[3][:, :, :half]))
-        nc.scalar.copy(out=y[3][:, :, :half], in_=acc3[:])
+        rounded3 = round_psum(3 * STORE, half, acc3)
         acc4 = second_product(3 * STORE + half, half, weigh(3 * STORE + half, half, th[3][:, :, half:]))
         rounded4 = round_psum(3 * STORE + half, half, acc4)
+        nc.scalar.copy(out=y[3][:, :, :half], in_=acc3[:])
         nc.scalar.copy(out=y[3][:, :, half:], in_=acc4[:])
         store_rows(3 * STORE, y[3])
         for c in range(3):
             planes(c * STORE, STORE, round_sbuf(c * STORE, STORE, y[c][:]))
         store_words(nc.scalar, 0, 3 * STORE)
-        planes(3 * STORE, half, round_sbuf(3 * STORE, half, y[3][:, :, :half]))
+        planes(3 * STORE, half, rounded3)
         planes(3 * STORE + half, half, rounded4)
         store_words(nc.sync, 3 * STORE, PICKED)
 

@@ -30,8 +30,8 @@ QUERY_GATHERS = (GROUPS[0], PICKED - GROUPS[0])
 FLOPS = 2 * 2 * 512 * 512 * 512
 
 
-def deal(nc, dst, src, run):
-    nc.vector.tensor_copy(
+def deal(engine, dst, src, run):
+    engine.tensor_copy(
         out=dst.rearrange("p (t c i) -> p c t i", t=PACK, i=run),
         in_=src.rearrange("p (c i t) -> p c t i", t=PACK, i=run),
     )
@@ -63,11 +63,12 @@ def tile_picked_sigattn_tanh_po_kernel(
         x_word_table = shared.tile([P, TABLE], U32, name="x_word_table", align_bytes=64, offset=0)
         kb_sb = tile("kb_sb", [P, PACK], F32)
         gn_sb = tile("gn_sb", [P, PACK], F32)
+        held_bias = shared.tile([P, 1], F32, name="held_bias", align_bytes=64, offset=4 * TABLE)
 
-        mx_scales = tile("mx_scales", [P, 3 * PICKED], U8)
+        mx_scales = tile("mx_scales", [P, 4 * PICKED], U8)
         nc.vector.memset(d_scale_table[:].bitcast(I32), 0)
         nc.vector.memset(x_scale_table[:].bitcast(I32), 0)
-        nc.vector.memset(mx_scales[:, 2 * PICKED :].bitcast(I32), 0)
+        nc.vector.memset(mx_scales[:, 3 * PICKED :].bitcast(I32), 0)
 
         nc.sync.dma_start(kidx_sb[:], kidx)
         nc.sync.dma_start(offs_sb[:], offs)
@@ -77,21 +78,23 @@ def tile_picked_sigattn_tanh_po_kernel(
         nc.scalar.dma_start(d_scale_table[:].bitcast(I32)[row_places, :], d_scales[0].bitcast(I32))
         nc.scalar.dma_start(kb_sb[:], kb.rearrange("(p t) o -> p (t o)", t=PACK))
         nc.scalar.dma_start(x_scale_table[:].bitcast(I32)[row_places, :], x_scales[0].bitcast(I32))
-        nc.scalar.dma_start(mx_scales[:, 2 * PICKED :].bitcast(I32)[row_places, :], w1_scales[0].bitcast(I32))
+        nc.scalar.dma_start(mx_scales[:, 3 * PICKED :].bitcast(I32)[row_places, :], w1_scales[0].bitcast(I32))
         nc.scalar.dma_start(d_word_table[:, 256:].bitcast(I32), d_words_hbm[:, 256:])
         nc.scalar.dma_start(x_word_table[:].bitcast(I32), x_words[0].rearrange("p n t -> p (n t)").bitcast(I32))
         nc.scalar.dma_start(gn_sb[:], gn.rearrange("(p t) o -> p (t o)", t=PACK))
+        nc.scalar.copy(out=held_bias[:], in_=kb_sb[:, 0:1])
 
         d_scale_picked = tile("d_scale_picked", [P, PICKED], U8)
         x_scale_picked = tile("x_scale_picked", [P, PICKED], U8, tag="x_picked")
         nc.vector.tensor_copy(d_scale_picked[:], d_scale_table[:].indirect(kidx_sb[:]))
         nc.vector.tensor_copy(x_scale_picked[:], x_scale_table[:].indirect(offs_sb[:]))
-        deal(nc, mx_scales[:, :PICKED], d_scale_picked[:], byte_run)
+        deal(nc.gpsimd, mx_scales[:, 2 * PICKED : 3 * PICKED], mx_scales[:, 3 * PICKED :], byte_run)
+        deal(nc.vector, mx_scales[:, :PICKED], d_scale_picked[:], byte_run)
         nc.vector.tensor_copy(mx_scales[:, PICKED : 2 * PICKED].bitcast(I32), x_scale_picked[:].bitcast(I32))
         for r in range(1, QUADRANT // BLOCK_PARTITIONS):
             nc.sync.dma_start(
-                mx_scales[:].bitcast(I32)[r:P:QUADRANT, :],
-                mx_scales[:].bitcast(I32)[BLOCK_PARTITIONS * r : P : QUADRANT, :],
+                mx_scales[:, : 3 * PICKED].bitcast(I32)[r:P:QUADRANT, :],
+                mx_scales[:, : 3 * PICKED].bitcast(I32)[BLOCK_PARTITIONS * r : P : QUADRANT, :],
             )
         w_word_in = tile("w_word_in", [P, PICKED], U32, tag="x_picked")
         nc.sync.dma_start(w_word_in[:].bitcast(I32), w1_words[0].rearrange("p n t -> p (n t)").bitcast(I32))
@@ -101,7 +104,7 @@ def tile_picked_sigattn_tanh_po_kernel(
         d_word_picked = tile("d_word_picked", [P, PICKED], U32, tag="d_words")
         key_words = tile("key_words", [P, PICKED], U32)
         nc.vector.tensor_copy(d_word_picked[:], d_word_table[:].indirect(kidx_sb[:]))
-        deal(nc, key_words[:].bitcast(I32), d_word_picked[:].bitcast(I32), word_run)
+        deal(nc.vector, key_words[:].bitcast(I32), d_word_picked[:].bitcast(I32), word_run)
 
         early, late = QUERY_GATHERS
         early_words = tile("early_words", [P, early], U32)
@@ -111,10 +114,8 @@ def tile_picked_sigattn_tanh_po_kernel(
         query_groups = [early_words[:]]
         for g in range(1, len(GROUPS)):
             query_groups.append(late_words[:, sum(GROUPS[1:g]) : sum(GROUPS[1 : g + 1])])
-        value_words = shared.tile([P, PICKED], U32, name="value_words", align_bytes=64, offset=0)
-        value_scales = shared.tile([P, PICKED], U8, name="value_scales", align_bytes=64, offset=4 * PICKED)
-        deal(nc, value_scales[:], mx_scales[:, 2 * PICKED :], byte_run)
-        deal(nc, value_words[:].bitcast(I32), w_word_in[:].bitcast(I32), word_run)
+        value_words = shared.tile([P, PICKED], U32, name="value_words", align_bytes=64, offset=4 * TABLE)
+        value_scales = mx_scales[:, 2 * PICKED : 3 * PICKED]
 
         out_rows = out_0.rearrange("(p t) j -> p t j", t=PACK)
         out_words_hbm = out_1[0].rearrange("p n t -> p (n t)").bitcast(I32)
@@ -139,9 +140,8 @@ def tile_picked_sigattn_tanh_po_kernel(
                         stop=True,
                     )
                 for t in range(t0, t0 + per_bank):
-                    nc.scalar.activation(
-                        out=th[:, t, :], in_=scores[:, t - t0, :], func=ACT.Tanh, bias=kb_sb[:, t : t + 1], scale=0.0625
-                    )
+                    bias = held_bias[:] if (g, t) == (1, 0) else kb_sb[:, t : t + 1]
+                    nc.scalar.activation(out=th[:, t, :], in_=scores[:, t - t0, :], func=ACT.Tanh, bias=bias, scale=0.0625)
             return th
 
         def weigh(j0, width, th):
@@ -197,7 +197,9 @@ def tile_picked_sigattn_tanh_po_kernel(
         th = [tanh_group(g) for g in range(3)]
         y = [tile("y%d" % c, [P, PACK, STORE], F32) for c in range(PICKED // STORE)]
         half = STORE // 2
-        acc0 = second_product(0, STORE, weigh(0, STORE, th[0][:]))
+        z0 = weigh(0, STORE, th[0][:])
+        deal(nc.vector, value_words[:].bitcast(I32), w_word_in[:].bitcast(I32), word_run)
+        acc0 = second_product(0, STORE, z0)
         nc.scalar.copy(out=y[0][:], in_=acc0[:])
         store_rows(0, y[0])
         th.append(tanh_group(3))

@@ -26,7 +26,7 @@ FIRST_BANKS = (1, 1, 2)
 LATER_BANKS = (2, 2)
 SCORE_BANKS = 5
 RESULT_BANKS = 3
-QUERY_GATHERS = (GROUPS[0], PICKED - GROUPS[0])
+QUERY_GATHERS = (GROUPS[0], GROUPS[1], PICKED - GROUPS[0] - GROUPS[1])
 FLOPS = 2 * 2 * 512 * 512 * 512
 
 
@@ -106,14 +106,16 @@ def tile_picked_sigattn_tanh_po_kernel(
         nc.vector.tensor_copy(d_word_picked[:], d_word_table[:].indirect(kidx_sb[:]))
         deal(nc.vector, key_words[:].bitcast(I32), d_word_picked[:].bitcast(I32), word_run)
 
-        early, late = QUERY_GATHERS
+        early, second, late = QUERY_GATHERS
         early_words = tile("early_words", [P, early], U32)
+        second_words = tile("second_words", [P, second], U32)
         late_words = tile("late_words", [P, late], U32)
         nc.vector.tensor_copy(early_words[:], x_word_table[:].indirect(list_part(offs_sb, 0, early)))
-        nc.vector.tensor_copy(late_words[:], x_word_table[:].indirect(list_part(offs_sb, early, late)))
-        query_groups = [early_words[:]]
-        for g in range(1, len(GROUPS)):
-            query_groups.append(late_words[:, sum(GROUPS[1:g]) : sum(GROUPS[1 : g + 1])])
+        nc.vector.tensor_copy(second_words[:], x_word_table[:].indirect(list_part(offs_sb, early, second)))
+        nc.vector.tensor_copy(late_words[:], x_word_table[:].indirect(list_part(offs_sb, early + second, late)))
+        query_groups = [early_words[:], second_words[:]]
+        for g in range(2, len(GROUPS)):
+            query_groups.append(late_words[:, sum(GROUPS[2:g]) : sum(GROUPS[2 : g + 1])])
         value_words = shared.tile([P, PICKED], U32, name="value_words", align_bytes=64, offset=4 * TABLE)
         value_scales = mx_scales[:, 2 * PICKED : 3 * PICKED]
 

from contextlib import ExitStack

import concourse.mybir as mybir

F32 = mybir.dt.float32
BF16 = mybir.dt.bfloat16
I32 = mybir.dt.int32
U32 = mybir.dt.uint32
U16 = mybir.dt.uint16
U8 = mybir.dt.uint8
FP8X4 = mybir.dt.float8_e4m3fn_x4
ACT = mybir.ActivationFunctionType
ALU = mybir.AluOpType

P = 128
PACK = 4
TABLE = 2048
PICKED = 512
LIST_GROUP = 16
BLOCK_PARTITIONS = 8
QUADRANT = 32
LINE_BYTES = 16
STORE = 128
GROUPS = (128, 128, 128, 128)
FIRST_BANKS = (1, 1, 2)
LATER_BANKS = (2, 2)
SCORE_BANKS = 5
RESULT_BANKS = 3
QUERY_GATHERS = (GROUPS[0], GROUPS[1], PICKED - GROUPS[0] - GROUPS[1])
FLOPS = 2 * 2 * 512 * 512 * 512


def deal(engine, dst, src, run):
    engine.tensor_copy(
        out=dst.rearrange("p (t c i) -> p c t i", t=PACK, i=run),
        in_=src.rearrange("p (c i t) -> p c t i", t=PACK, i=run),
    )


def list_part(offsets, start, count):
    return offsets[:, start // LIST_GROUP : (start + count) // LIST_GROUP]


def tile_picked_sigattn_tanh_po_kernel(
    tc, x_words, x_scales, d_words, d_scales, kb, gn, w1_words, w1_scales, offs, kidx, out_0, out_1, out_2
):
    nc = tc.nc
    byte_run = LINE_BYTES
    word_run = LINE_BYTES // 4
    with ExitStack() as ctx:
        sb = ctx.enter_context(tc.tile_pool(name="sb", bufs=1))
        shared = ctx.enter_context(tc.tile_pool(name="shared", bufs=1))
        ps = ctx.enter_context(tc.psum_pool(name="ps", bufs=1))

        def tile(name, shape, dtype, tag=None):
            return sb.tile(shape, dtype, name=name, tag=tag or name, align_bytes=64)

        kidx_sb = sb.tile([P, PICKED // LIST_GROUP], U16, name="kidx_sb")
        offs_sb = sb.tile([P, PICKED // LIST_GROUP], U16, name="offs_sb")
        d_scale_table = tile("d_scale_table", [P, TABLE], U8)
        x_scale_table = tile("x_scale_table", [P, TABLE], U8, tag="d_words")
        d_word_table = tile("d_word_table", [P, TABLE], U32)
        x_word_table = shared.tile([P, TABLE], U32, name="x_word_table", align_bytes=64, offset=0)
        kb_sb = tile("kb_sb", [P, PACK], F32)
        gn_sb = tile("gn_sb", [P, PACK], F32)
        held_bias = shared.tile([P, 1], F32, name="held_bias", align_bytes=64, offset=4 * TABLE)

        mx_scales = tile("mx_scales", [P, 4 * PICKED], U8)
        nc.vector.memset(d_scale_table[:].bitcast(I32), 0)
        nc.vector.memset(x_scale_table[:].bitcast(I32), 0)
        nc.vector.memset(mx_scales[:, 3 * PICKED :].bitcast(I32), 0)

        nc.sync.dma_start(kidx_sb[:], kidx)
        nc.sync.dma_start(offs_sb[:], offs)
        d_words_hbm = d_words[0].rearrange("p n t -> p (n t)").bitcast(I32)
        row_places = slice(0, P, BLOCK_PARTITIONS)
        nc.scalar.dma_start(d_word_table[:, :256].bitcast(I32), d_words_hbm[:, :256])
        nc.scalar.dma_start(d_scale_table[:].bitcast(I32)[row_places, :], d_scales[0].bitcast(I32))
        nc.scalar.dma_start(kb_sb[:], kb.rearrange("(p t) o -> p (t o)", t=PACK))
        nc.scalar.dma_start(x_scale_table[:].bitcast(I32)[row_places, :], x_scales[0].bitcast(I32))
        nc.scalar.dma_start(mx_scales[:, 3 * PICKED :].bitcast(I32)[row_places, :], w1_scales[0].bitcast(I32))
        nc.scalar.dma_start(d_word_table[:, 256:].bitcast(I32), d_words_hbm[:, 256:])
        nc.scalar.dma_start(x_word_table[:].bitcast(I32), x_words[0].rearrange("p n t -> p (n t)").bitcast(I32))
        nc.scalar.dma_start(gn_sb[:], gn.rearrange("(p t) o -> p (t o)", t=PACK))
        nc.scalar.copy(out=held_bias[:], in_=kb_sb[:, 0:1])

        d_scale_picked = tile("d_scale_picked", [P, PICKED], U8)
        x_scale_picked = tile("x_scale_picked", [P, PICKED], U8, tag="x_picked")
        nc.vector.tensor_copy(d_scale_picked[:], d_scale_table[:].indirect(kidx_sb[:]))
        nc.vector.tensor_copy(x_scale_picked[:], x_scale_table[:].indirect(offs_sb[:]))
        deal(nc.gpsimd, mx_scales[:, 2 * PICKED : 3 * PICKED], mx_scales[:, 3 * PICKED :], byte_run)
        deal(nc.vector, mx_scales[:, :PICKED], d_scale_picked[:], byte_run)
        nc.vector.tensor_copy(mx_scales[:, PICKED : 2 * PICKED].bitcast(I32), x_scale_picked[:].bitcast(I32))
        for r in range(1, QUADRANT // BLOCK_PARTITIONS):
            nc.sync.dma_start(
                mx_scales[:, : 3 * PICKED].bitcast(I32)[r:P:QUADRANT, :],
                mx_scales[:, : 3 * PICKED].bitcast(I32)[BLOCK_PARTITIONS * r : P : QUADRANT, :],
            )
        w_word_in = tile("w_word_in", [P, PICKED], U32, tag="x_picked")
        nc.sync.dma_start(w_word_in[:].bitcast(I32), w1_words[0].rearrange("p n t -> p (n t)").bitcast(I32))
        key_scales = mx_scales[:, :PICKED]
        query_scales = mx_scales[:, PICKED : 2 * PICKED]

        d_word_picked = tile("d_word_picked", [P, PICKED], U32, tag="d_words")
        key_words = tile("key_words", [P, PICKED], U32)
        nc.vector.tensor_copy(d_word_picked[:], d_word_table[:].indirect(kidx_sb[:]))
        deal(nc.vector, key_words[:].bitcast(I32), d_word_picked[:].bitcast(I32), word_run)

        early, second, late = QUERY_GATHERS
        early_words = tile("early_words", [P, early], U32)
        second_words = tile("second_words", [P, second], U32)
        late_words = tile("late_words", [P, late], U32)
        nc.vector.tensor_copy(early_words[:], x_word_table[:].indirect(list_part(offs_sb, 0, early)))
        nc.vector.tensor_copy(second_words[:], x_word_table[:].indirect(list_part(offs_sb, early, second)))
        nc.vector.tensor_copy(late_words[:], x_word_table[:].indirect(list_part(offs_sb, early + second, late)))
        query_groups = [early_words[:], second_words[:]]
        for g in range(2, len(GROUPS)):
            query_groups.append(late_words[:, sum(GROUPS[2:g]) : sum(GROUPS[2 : g + 1])])
        value_words = shared.tile([P, PICKED], U32, name="value_words", align_bytes=64, offset=4 * TABLE)
        value_scales = mx_scales[:, 2 * PICKED : 3 * PICKED]

        out_rows = out_0.rearrange("(p t) j -> p t j", t=PACK)
        out_words_hbm = out_1[0].rearrange("p n t -> p (n t)").bitcast(I32)
        out_scales = tile("out_scales", [P, PICKED], U8)
        out_words = tile("out_words", [P, PICKED], U32)

        def tanh_group(g):
            j0, width = sum(GROUPS[:g]), GROUPS[g]
            banks = FIRST_BANKS if g == 0 else LATER_BANKS
            th = tile("tanh%d" % j0, [P, PACK, width], F32)
            for b, per_bank in enumerate(banks):
                t0 = sum(banks[:b])
                scores = ps.tile([P, per_bank, width], F32, name="scores", bufs=SCORE_BANKS)
                for t in range(t0, t0 + per_bank):
                    nc.tensor.matmul_mx(
                        out=scores[:, t - t0, :],
                        lhsT=key_words[:, t * P : (t + 1) * P].bitcast(FP8X4),
                        lhsT_scale=key_scales[:, t * P : (t + 1) * P],
                        rhs=query_groups[g].bitcast(FP8X4),
                        rhs_scale=query_scales[:, j0 : j0 + width],
                        start=True,
                        stop=True,
                    )
                for t in range(t0, t0 + per_bank):
                    bias = held_bias[:] if (g, t) == (1, 0) else kb_sb[:, t : t + 1]
                    nc.scalar.activation(out=th[:, t, :], in_=scores[:, t - t0, :], func=ACT.Tanh, bias=bias, scale=0.0625)
            return th

        def weigh(j0, width, th):
            z = tile("z%d" % j0, [P, width * PACK], BF16)
            nc.vector.tensor_tensor(
                out=z[:].rearrange("p (c i t) -> p c t i", t=PACK, i=word_run),
                in0=th.rearrange("p t (c i) -> p c t i", i=word_run),
                in1=gn_sb[:].unsqueeze(1).unsqueeze(3).to_broadcast([P, width // word_run, PACK, word_run]),
                op=ALU.mult,
            )
            return z

        def second_product(j0, width, z):
            z_words = tile("z_words%d" % j0, [P, width], U32)
            z_scales = tile("z_scales%d" % j0, [P, width], U8)
            nc.vector.quantize_mx(out=z_words[:].bitcast(FP8X4), scales=z_scales[:], in_=z[:])
            acc = ps.tile([P, PACK, width], F32, name="acc", bufs=RESULT_BANKS)
            for t in range(PACK):
                nc.tensor.matmul_mx(
                    out=acc[:, t, :],
                    lhsT=value_words[:, t * P : (t + 1) * P].bitcast(FP8X4),
                    lhsT_scale=value_scales[:, t * P : (t + 1) * P],
                    rhs=z_words[:].bitcast(FP8X4),
                    rhs_scale=z_scales[:],
                    start=True,
                    stop=True,
                )
            return acc

        def round_sbuf(j0, width, y):
            rounded = tile("yb%d" % j0, [P, width * PACK], BF16)
            nc.vector.tensor_copy(
                out=rounded[:].rearrange("p (c i t) -> p c t i", t=PACK, i=word_run),
                in_=y.rearrange("p t (c i) -> p c t i", i=word_run),
            )
            return rounded

        def round_psum(j0, width, acc):
            rounded = tile("yb%d" % j0, [P, width * PACK], BF16)
            nc.scalar.copy(out=rounded[:].rearrange("p (j t) -> p j t", t=PACK), in_=acc[:].rearrange("p t j -> p j t"))
            return rounded

        def planes(j0, width, rounded):
            cols = slice(j0, j0 + width)
            nc.vector.quantize_mx(out=out_words[:, cols].bitcast(FP8X4), scales=out_scales[:, cols], in_=rounded[:])

        def store_rows(j0, y):
            nc.sync.dma_start(out_rows[:, :, j0 : j0 + STORE], y[:])

        def store_words(queue, j0, j1):
            queue.dma_start(out_words_hbm[:, j0:j1], out_words[:, j0:j1].bitcast(I32))

        th = [tanh_group(g) for g in range(3)]
        y = [tile("y%d" % c, [P, PACK, STORE], F32) for c in range(PICKED // STORE)]
        half = STORE // 2
        z0 = weigh(0, STORE, th[0][:])
        deal(nc.vector, value_words[:].bitcast(I32), w_word_in[:].bitcast(I32), word_run)
        acc0 = second_product(0, STORE, z0)
        nc.scalar.copy(out=y[0][:], in_=acc0[:])
        store_rows(0, y[0])
        th.append(tanh_group(3))
        for c in (1, 2):
            acc = second_product(c * STORE, STORE, weigh(c * STORE, STORE, th[c][:]))
            nc.scalar.copy(out=y[c][:], in_=acc[:])
            store_rows(c * STORE, y[c])
        acc3 = second_product(3 * STORE, half, weigh(3 * STORE, half, th[3][:, :, :half]))
        rounded3 = round_psum(3 * STORE, half, acc3)
        acc4 = second_product(3 * STORE + half, half, weigh(3 * STORE + half, half, th[3][:, :, half:]))
        rounded4 = round_psum(3 * STORE + half, half, acc4)
        nc.scalar.copy(out=y[3][:, :, :half], in_=acc3[:])
        nc.scalar.copy(out=y[3][:, :, half:], in_=acc4[:])
        store_rows(3 * STORE, y[3])
        for c in range(3):
            planes(c * STORE, STORE, round_sbuf(c * STORE, STORE, y[c][:]))
        store_words(nc.scalar, 0, 3 * STORE)
        planes(3 * STORE, half, rounded3)
        planes(3 * STORE + half, half, rounded4)
        store_words(nc.sync, 3 * STORE, PICKED)

        rows = QUADRANT // BLOCK_PARTITIONS
        for q in range(P // QUADRANT):
            queue = nc.scalar if q % 2 == 0 else nc.sync
            queue.dma_start(
                out_2[0].bitcast(I32)[rows * q : rows * (q + 1), :],
                out_scales[:].bitcast(I32)[QUADRANT * q : QUADRANT * q + rows, :],
            )
